import numpy as np, ml_dtypes
CORES = [5,29,101,125,133,157,229,253]
N = 8
import mx_ref
BF = ml_dtypes.bfloat16
def gcols(t, e):
    v = np.concatenate([t.reshape(8, 16, -1, 4), np.zeros((8, 16, 1, 4), BF)], axis=2)
    return np.ascontiguousarray(np.stack([v[g][:, e[g]] for g in range(8)])).reshape(128, -1)
def tile(rs):
    return np.stack(rs, axis=2).reshape(128, -1).astype(BF)
def cut(t, i, w=512):
    return t[:, w * i:w * i + w]
def pick(q, e):
    c = np.concatenate([q[0].reshape(128, -1, 4), np.zeros((128, 1, 4), np.uint8)], axis=1); s = np.concatenate([q[1], np.ones((16, 1), np.uint8)], axis=1)
    return (np.ascontiguousarray(c[:, e].reshape(128, -1)), np.ascontiguousarray(s[:, e]))
def join(*qs):
    return (np.concatenate([q[0] for q in qs], axis=1), np.concatenate([q[1] for q in qs], axis=1))
def put(q, e, v):
    c, s = q[0].reshape(128, -1, 4).copy(), q[1].copy(); c[:, e] = v[0].reshape(128, -1, 4); s[:, e] = v[1]
    return (c.reshape(128, -1), s)
def pk(c, s):
    return (np.ascontiguousarray(c), mx_ref.live(s))
def emit(q):
    return q[0], q[1]
def packed(v, rng):
    q = [mx_ref.quantize(np.ascontiguousarray(v[r])) for r in range(N)]
    return np.stack([a for a, b in q]), np.stack([mx_ref.plane(b, rng) for a, b in q])
def values_of_codes():
    e, c = np.zeros((128, 128, 4), np.float32), np.zeros((128, 2, 4), np.uint8)
    e[np.arange(128), np.arange(128), 0] = 1
    c[:127, :, 0] = np.arange(256).reshape(2, 128).T[:127]
    return mx_ref.matmul(mx_ref.quantize(e.reshape(128, 512).astype(BF)), (c.reshape(128, 8), np.full((16, 2), 127, np.uint8))).T.reshape(-1).astype(np.float64)
CODE_VALUE, SCALE_VALUE = values_of_codes(), 2.0 ** (np.arange(256) - 127.0)
def decode(q):
    return (CODE_VALUE[q[0]].reshape(16, 8, -1, 4) * SCALE_VALUE[q[1]][:, None, :, None] + 0.0).reshape(128, -1).astype(np.float32)
def f(rng, *shape):
    return mx_ref.flush((rng.standard_normal(shape, dtype=np.float32) * np.exp2(rng.integers(-2, 3, shape[:-1] + (1,)))).astype(BF))
def wide(rng, *shape, cols=0):
    v = rng.standard_normal(shape, dtype=np.float32) * np.exp2(rng.integers(-12, 13, shape)).astype(np.float32)
    if cols: v *= np.repeat(np.exp2(rng.integers(-cols, cols + 1, shape[:-2] + (1, shape[-1] // 4))) * (rng.random(shape[:-2] + (1, shape[-1] // 4)) > 0.0625), 4, axis=-1).astype(np.float32)
    return mx_ref.flush(v.astype(BF))
C, K, R = 448, 32, 3
def order(p):
    return np.argsort(-(p[::16] + np.float32(0.0)), axis=1, kind="stable")
def numbers_of(rng):
    return {"x": np.array(f(rng, N, 128, 4 * C)), "u": np.array(f(rng, N, 128, 512)), "v": np.array(f(rng, N, 128, 512))}
def weights(rng, w):
    c, p = packed(w, rng)
    return {"wc": c, "ws": p}
def still(rng):
    w = np.zeros((N, 128, 4, 128, 4), np.float32)
    i = np.arange(128)
    for b in range(4): w[:, i, b, i, b] = 32
    return weights(rng, w.reshape(N, 128, 2048).astype(BF))
def signs(rng):
    return np.stack([rng.permutation(8) % 2 * 2.0 - 1.0 for r in range(N)])
def setup_inputs(rng):
    return {**numbers_of(rng), **weights(rng, f(rng, N, 128, 2048))}
def setup_inputs_ties(rng):
    d = numbers_of(rng)
    e = rng.permutation(N)
    x = d["x"].reshape(N, 8, 16, C, 4)
    for r in range(N):
        k = np.zeros(C, int) if r == e[0] else rng.permutation(C) % 3
        a = x[r][:, :8, :3].copy()
        a[:, :, 2] = 0
        x[r][:, :8] = a[:, :, k]
    x[e[1]] = 0
    u = d["u"].reshape(N, 8, 16, 128, 4)
    u[:, :, 8:, ::16] = 0
    w = np.array(f(rng, N, 128, 2048)).reshape(N, 8, 16, 4, 8, 16, 4)
    w[:, :, 8:, :, :, :8] = 0
    return {"x": x.reshape(N, 128, 4 * C), "u": u.reshape(N, 128, 512), "v": d["v"], **weights(rng, w.reshape(N, 128, 2048))}
def setup_inputs_near(rng):
    d = numbers_of(rng)
    x = d["x"].astype(np.float32).reshape(N, 8, 16, C, 4)
    s = np.arange(C) // 2
    g = ((s[:, None] >> np.arange(8)) & 1) * np.exp2(np.arange(8) - 23.0)
    x[:, :, 0] = 0
    x[:, :, 0, :, 0] = signs(rng)[:, :, None]
    x[:, :, 8] = g[:, :4]
    x[:, :, 9] = g[:, 4:]
    x[:, :, 10:] = rng.integers(4, 8, (N, 8, 6, C, 4)) * rng.choice([-1.0, 1.0], (N, 8, 6, C, 4)) * 2.0 ** -20
    u = d["u"].reshape(N, 128, 128, 4)
    k = np.where(rng.permutation(N) < N // 2, 2.0 ** -30, 1.0).astype(np.float32).astype(BF)
    u[:, :, ::16] = 0
    for h in range(0, 128, 16):
        u[:, h, h, 0] = k
        u[:, h + 8:h + 10, h] = k[:, None, None]
    return {"x": x.reshape(N, 128, 4 * C).astype(BF), "u": u.reshape(N, 128, 512), "v": d["v"], **still(rng)}
def setup_inputs_huge(rng):
    d = numbers_of(rng)
    x = 2.0 ** 30 * (0.6 + 0.4 * rng.random((N, 128, C, 4)))
    c = np.stack([rng.permutation(C) % 2 * 2.0 - 1.0 for r in range(N)])
    c[rng.permutation(N) < N // 2] = 1
    x *= c[:, None, :, None]
    u = d["u"].reshape(N, 128, 128, 4)
    a = 2.0 ** 30 * (1 - 0.25 * rng.random((N, 128, 8, 4))) * signs(rng)[:, None, :, None]
    u[:, :, ::16] = a.astype(np.float32).astype(BF)
    return {"x": x.astype(np.float32).reshape(N, 128, 4 * C).astype(BF), "u": u.reshape(N, 128, 512), "v": d["v"], **still(rng)}
def setup_inputs_spread(rng):
    d = setup_inputs(rng)
    d["x"] = wide(rng, N, 128, 4 * C, cols=6)
    return d
def check_inputs(d):
    b = []
    for k in ("x", "u", "v"):
        a = np.abs(d[k].astype(np.float32))
        if not (np.isfinite(a).all() and ((a == 0) | (a >= 2.0 ** -30) & (a <= 2.0 ** 30)).all()): b.append("a value of " + k)
    return b
def reference(x, u, v, wc, ws):
    qu = [mx_ref.quantize(u[r]) for r in range(N)]
    lay = [pk(wc[r], ws[r]) for r in range(N)]
    now = [x[r] for r in range(N)]
    place = np.tile(C + np.arange(K), (8, 1))
    for t in range(R):
        made, o, border = [], [], []
        for r in range(N):
            q = mx_ref.quantize(now[r])
            made.append(tile([mx_ref.matmul(pick(lay[r], np.arange(128 * b, 128 * b + 128)), q) * np.float32(0.03125) for b in range(4)]))
            o.append(order(mx_ref.matmul(qu[r], mx_ref.quantize(made[r]))))
            border.append(mx_ref.quantize(gcols(made[r], o[r][:, :K])))
        came = decode(join(*border)).astype(BF)
        for r in range(N):
            e = np.concatenate([o[r], place], axis=1)
            i = np.argsort(o[r], axis=1)
            now[r] = gcols(np.concatenate([made[r], cut(came, (r + 1) % N, 4 * K)], axis=1), np.take_along_axis(e, i + K, axis=1))
    y, ol = np.zeros((N, 128, C), np.float32), np.zeros((N, 8, C), np.float32)
    oc, osc = np.zeros((N, 128, 4 * C), np.uint8), np.zeros((N, 16, C), np.uint8)
    for r in range(N):
        q = mx_ref.quantize(now[r])
        y[r] = mx_ref.matmul(mx_ref.quantize(v[r]), q)
        ol[r] = o[r]
        oc[r], osc[r] = emit(q)
    return {"y": y, "ol": ol, "oc": oc, "osc": osc}

@@ -1,0 +1,480 @@
+from concourse.bass import DstId, RemoteDMATransfer
+from concourse.mybir import dt, AluOpType, ActivationFunctionType, AxisListType
+
+C, K, ROUNDS = 448, 32, 3
+H = C // 2
+NSEG = C // 16
+NA = 7
+NR = 2
+SHORT = 56
+CA = 256
+BIG = 2.0 ** 90
+CODE = "float8_e4m3fn_x4"
+
+
+def row_words(m):
+    return 4 * m if m else C // 4
+
+
+def blocks():
+    longs = [0] + list(range(NSEG - 1 - NA, NSEG // 2, -1)) + list(range(NSEG - 1, NSEG - 1 - NA, -1))
+    out, w = [], 0
+    for i, lg in enumerate(longs):
+        n = SHORT + max(row_words(lg), 128 - SHORT)
+        out.append((NSEG // 2 - i, lg, w, n))
+        w += n
+    return out, w
+
+
+BLOCKS, NW = blocks()
+A_ROWS = list(range(NSEG - NA, NSEG))
+ORDER = [(x[0], x[1:]) if x[0] in "mh" else (x[0], int(x[1:])) for x in (
+    "ma ha mb p23 hb p22 r0 r17 r7 r10 r20 r14 r23 p21 r9 r18 r19 q0 r4 w0 p25 p24 r21 p27 r11 p26 c0 r22 r12 r13 r26 q4 q2 w4 r27 s0 q1 w1 q3 "
+    "s14 w3 c3 r25 r16 r24 s13 r15 c2 w2 c4 s20 q7 c7 r8 r3 r1 s18 c1 q5 r6 w5 s6 s7 q6 s17 s11 c5 r5 s3 w6 r2 q8 q9 c6 s10 q10 s8 s5 q11 c8 c9 "
+    "q12 q13 c10 s19 s2 c11 s12 c12 c13 s15 s9 s4 s16 s1").split()]
+
+SCRATCH = {
+    "x0": ("sbuf", [128, 4 * C], "bfloat16"), "xs": ("sbuf", [128, 4 * C], "bfloat16"), "ys": ("sbuf", [128, 4 * C], "bfloat16"),
+    "qx": ("sbuf", [128, C], CODE), "sx": ("sbuf", [128, C], "uint8"),
+    "wq": ("sbuf", [128, 512], CODE), "wp": ("sbuf", [128, 512], "uint8"),
+    "ut": ("sbuf", [128, 512], "bfloat16"), "qu": ("sbuf", [128, 128], CODE), "su": ("sbuf", [128, 128], "uint8"),
+    "qus": ("sbuf", [128, 128], CODE), "sus": ("sbuf", [128, 128], "uint8"),
+    "vt": ("sbuf", [128, 512], "bfloat16"), "qv": ("sbuf", [128, 128], CODE), "sv": ("sbuf", [128, 128], "uint8"),
+    "mm": ("sbuf", [128, C], "float32"), "hh": ("sbuf", [128, C], "float32"),
+    "fl": ("sbuf", [128, 4 * NW], "bfloat16"), "qf": ("sbuf", [128, NW], CODE), "sf": ("sbuf", [128, NW], "uint8"),
+    "tmp": ("sbuf", [128, 16 * sum(A_ROWS)], "bfloat16"), "junk": ("sbuf", [128, (NSEG - NA) * 112], "bfloat16"),
+    "a1": ("sbuf", [128, C], "float32"), "a2": ("sbuf", [128, C], "float32"),
+    "offi": ("sbuf", [128, 32], "uint16"), "oo": ("sbuf", [128, C + K], "float32"),
+    "g1": ("sbuf", [128, C], "float32"), "g2": ("sbuf", [128, C], "float32"), "offx": ("sbuf", [128, C // 4], "uint16"),
+    "l1": ("sbuf", [128, 2 * K], "float32"), "l2": ("sbuf", [128, 2 * K], "float32"), "offs": ("sbuf", [128, 16], "uint16"),
+    "da": ("sbuf", [128, 2 * C], "bfloat16"), "db": ("sbuf", [128, 2 * C], "bfloat16"), "gg": ("sbuf", [128, 4 * K], "bfloat16"),
+    "yo": ("sbuf", [128, C], "float32"), "olb": ("sbuf", [128, C], "float32"),
+    "pi": ("sbuf", [128, 8], "int32"), "pc": ("sbuf", [128, 16], "float32"),
+    "ui": ("sbuf", [128, 8], "int32"), "uoff": ("sbuf", [128, 16], "uint16"),
+    "dd": ("sbuf", [128, 512], "bfloat16"), "dabs": ("sbuf", [128, 512], "bfloat16"), "cv": ("sbuf", [128, 512], "bfloat16"),
+    "ct": ("sbuf", [128, 6 * 512], "bfloat16"), "qc": ("sbuf", [128, 6 * 128], CODE), "sc": ("sbuf", [128, 6 * 128], "uint8"),
+    "n16": ("sbuf", [128, C], "bfloat16"), "n4": ("sbuf", [128, C], "bfloat16"), "n8": ("sbuf", [128, K], "bfloat16"),
+    "maska": ("sbuf", [128, C], "bfloat16"), "cseg": ("sbuf", [128, C], "bfloat16"), "keep16": ("sbuf", [128, C], "bfloat16"),
+    "keep4": ("sbuf", [128, C], "bfloat16"), "mask4": ("sbuf", [128, C], "bfloat16"),
+    "keep8": ("sbuf", [128, K], "bfloat16"), "mask8": ("sbuf", [128, K], "bfloat16"),
+    "jj": ("sbuf", [128, C], "float32"), "kio": ("sbuf", [128, 32], "float32"), "zt": ("sbuf", [128, 4 * SHORT], "bfloat16"),
+}
+for _t in range(ROUNDS):
+    SCRATCH["qy%d" % _t] = ("sbuf", [128, C], CODE)
+    SCRATCH["sy%d" % _t] = ("sbuf", [128, C], "uint8")
+    SCRATCH["lq%d" % _t] = ("sbuf", [128, C], CODE)
+    SCRATCH["lp%d" % _t] = ("sbuf", [128, C], "uint8")
+    SCRATCH["lo%d" % _t] = ("sbuf", [128, 16], "uint16")
+    SCRATCH["ll%d" % _t] = ("sbuf", [128, 16], "uint16")
+for _b in range(8):
+    SCRATCH["ps%d" % _b] = ("psum", [128, 512], "float32")
+
+SEMAPHORES = (["sV", "sA", "sP", "sG", "st", "left"] + ["ld%d" % i for i in range(7)]
+              + ["%s%d" % (s, t) for s in ("ra", "rl", "ba", "la") for t in range(ROUNDS)])
+
+A_, F_ = AluOpType, ActivationFunctionType
+
+
+def bits(engines):
+    return sum(1 << e for e in engines)
+
+
+def relays(T, topo, r):
+    src, dst = T.cores[r], T.cores[(r - 1) % len(T.cores)]
+    can = [d for d in topo.cores_of(src) if d != src and topo.may_write(d, dst)]
+    return sorted(can, key=lambda d: (topo.die(d) != topo.die(src), d))[:4], dst
+
+
+def pieces(t):
+    q = C // 4
+    return [("qy%d" % t, "lq%d" % t, q * i, q * i + q, i) for i in range(4)] + [("sy%d" % t, "lp%d" % t, 0, C, 2)]
+
+
+def side(T, name, a, b):
+    v = T[name][:, a:b]
+    return v.bitcast(dt.uint8) if SCRATCH[name][2] == CODE else v
+
+
+def relay_program(g, core, T, topo):
+    for r, c in enumerate(T.cores):
+        if core in topo.cores_of(c):
+            rel, dst = relays(T, topo, r)
+            if core not in rel:
+                return
+            k = rel.index(core)
+            on, off = topo.engines(c, core), topo.engines(core, dst)
+            rid, pid = topo.addr(dst, core)
+            for t in range(ROUNDS):
+                mine = [p for p in pieces(t) if p[4] == k]
+                g.wait_ge(T.sem["ra%d" % t], len(on) // 4 + (len(mine) - 1) * len(on))
+                e = len(off) // len(mine)
+                g.remote_dma_fused([RemoteDMATransfer(dst_ids=[DstId(rid=rid, pnc=pid)], dma_engine_mask=bits(off[e * i:e * i + e]),
+                                                      remote_sem=T.sem["ba%d" % t], src=side(T, p[1], p[2], p[3]), dst=side(T, p[1], p[2], p[3]))
+                                    for i, p in enumerate(mine)], local_sem=T.sem.left)
+                if k == 0:
+                    g.wait_ge(T.sem["rl%d" % t], len(on))
+                    g.remote_dma(T["ll%d" % t][:, 0:4], T["ll%d" % t][:, 0:4], T.sem["la%d" % t], T.sem.left, pid, rid, bits(off))
+            g.wait_ge(T.sem.left, ROUNDS * len(off) * (2 if k == 0 else 1))
+            return
+
+
+def rank_program(g, core, T, topo):
+    rank = T.rank_of(core)
+    if rank is None:
+        relay_program(g, core, T, topo)
+        return
+    rel, _ = relays(T, topo, rank)
+    eng = {"V": g.vector, "A": g.scalar, "P": g.tensor, "G": g, "S": g.sync}
+    ops, hist, masks = [], {}, {}
+
+    def v(name, a=0, b=None, step=1):
+        return (name, a, SCRATCH[name][1][1] if b is None else b, step)
+
+    def ap(x):
+        return T[x[0]][:, x[1]:x[2]:x[3]] if x[3] != 1 else T[x[0]][:, x[1]:x[2]]
+
+    def span(x):
+        if SCRATCH[x[0]][0] == "psum":
+            return 1
+        if x[1:] not in masks:
+            masks[x[1:]] = sum(1 << i for i in range(x[1], x[2], x[3]))
+        return masks[x[1:]]
+
+    def op(e, fn, reads, writes, sem=None, val=None):
+        me, deps = len(ops), set()
+        for x, wr in [(x, False) for x in reads] + [(x, True) for x in writes]:
+            m, psum = span(x), SCRATCH[x[0]][0] == "psum"
+            for o, om, ow in hist.get(x[0], []):
+                if om & m and o != me:
+                    same = ops[o]["e"] == e
+                    if (psum and same and e == "P") or not (wr or ow or (psum and not same)):
+                        continue
+                    deps.add(o)
+            hist[x[0]] = [h for h in hist.get(x[0], []) if not (wr and h[1] & ~m == 0)] + [(me, m, wr)]
+        ops.append({"e": e, "fn": fn, "deps": deps, "sem": sem, "val": val})
+
+    def ts(out, in0, s1, op0, s2=None, op1=None):
+        rd = [in0] + [s for s in (s1, s2) if isinstance(s, tuple)]
+        a1, a2 = [ap(s) if isinstance(s, tuple) else s for s in (s1, s2)]
+        if op1 is None:
+            op("V", lambda q: q.tensor_scalar(ap(out), ap(in0), a1, None, op0), rd, [out])
+        else:
+            op("V", lambda q: q.tensor_scalar(ap(out), ap(in0), a1, a2, op0, op1), rd, [out])
+
+    def tt(out, in0, in1, o):
+        op("V", lambda q: q.tensor_tensor(ap(out), ap(in0), ap(in1), o), [in0, in1], [out])
+
+    def scan(out, d0, d1, o0, o1):
+        op("V", lambda q: q.tensor_tensor_scan(ap(out), ap(d0), ap(d1), 0.0, o0, o1), [d0, d1], [out])
+
+    def copy(out, in_):
+        op("V", lambda q: q.tensor_copy(ap(out), ap(in_)), [in_], [out])
+
+    def fill(out, c):
+        op("V", lambda q: q.memset(ap(out), c), [], [out])
+
+    def add_up(out, in_):
+        op("V", lambda q: q.tensor_reduce(ap(out), ap(in_), AxisListType.X, A_.add), [in_], [out])
+
+    def act(out, in_, f, bias=None, scale=None, accum=None):
+        kw = {}
+        if bias is not None:
+            kw["bias"] = ap(bias) if isinstance(bias, tuple) else bias
+        if scale is not None:
+            kw["scale"] = scale
+        if accum is not None:
+            kw["accum_out"] = ap(accum)
+        op("A", lambda q: q.activation(ap(out), ap(in_), f, **kw), [in_] + ([bias] if isinstance(bias, tuple) else []),
+           [out] + ([accum] if accum else []))
+
+    def gather(e, out, win, off):
+        if e == "V":
+            op(e, lambda q: q.tensor_copy(ap(out), ap(win).indirect(ap(off))), [win, off], [out])
+        else:
+            op(e, lambda q: q.activation(ap(out), ap(win).indirect(ap(off)), F_.Copy), [win, off], [out])
+
+    def scatter(win, off, in_):
+        op("V", lambda q: q.tensor_copy(ap(win).indirect(ap(off)), ap(in_)), [in_, off], [win])
+
+    def quant(q, s, src, a, b):
+        op("V", lambda e: e.quantize_mx(ap(v(q, a, b)), ap(v(s, a, b)), ap(v(src, 4 * a, 4 * b))),
+           [v(src, 4 * a, 4 * b)], [v(q, a, b), v(s, a, b)])
+
+    def mx(bank, lq, ls, la, rq, rs, a, b, start=True, stop=True):
+        out = v("ps%d" % bank, 0, b - a)
+        rd = [v(lq, la, la + 128), v(ls, la, la + 128), v(rq, a, b), v(rs, a, b)]
+        op("P", lambda e: e.matmul_mx(ap(out), ap(rd[0]), ap(rd[1]), ap(rd[2]), ap(rd[3]), start, stop), rd, [out])
+
+    def iota(out, pattern, base, cm):
+        if SCRATCH[out[0]][2] == "int32":
+            op("G", lambda q: q.iota(ap(out), pattern, base, cm), [], [out])
+        else:
+            op("G", lambda q: q.iota(ap(out), pattern, base, cm, allow_small_or_imprecise_dtypes=True), [], [out])
+
+    loads, stores = [0], [0]
+
+    def load(e, out, src, after=()):
+        o = ap(out).bitcast(dt.uint8) if SCRATCH[out[0]][2] == CODE else ap(out)
+        op(e, lambda q: q.dma_start(o, src), list(after), [out], sem="ld%d" % loads[0], val=16)
+        loads[0] += 1
+
+    def store(e, dst, src, reads):
+        op(e, lambda q: q.dma_start(dst, src), reads, [], sem="st", val=16)
+        stores[0] += 1
+
+    def ps(b, a, c):
+        return v("ps%d" % b, a, c)
+
+    def col(name, j):
+        return v(name, j, j + 1)
+
+    load("S", v("x0", 0, 4 * H), T.x[:, 0:4 * H])
+    load("A", v("wp"), T.ws[:])
+    load("A", v("wq", 0, 256), T.wc[:, 0:1024])
+    load("S", v("wq", 256, 512), T.wc[:, 1024:2048])
+    load("S", v("x0", 4 * H, 4 * C), T.x[:, 4 * H:4 * C])
+    load("A", v("ut"), T.u[:])
+
+    iota(col("pi", 0), [[0, 1]], 0, 1)
+    iota(v("dd"), [[1, 512]], 0, -4)
+    iota(v("n16"), [[0, NSEG], [1, 16]], 0, 0)
+    iota(v("ui"), [[16, 8]], 0, 0)
+    for t in range(4):
+        iota(v("cv", t, 512, 4), [[1, 8], [0, 4], [-8, 4]], 8 * t, 0)
+    iota(v("kio", 0, A_ROWS[0]), [[-16, A_ROWS[0]]], C - 16 - 16 * NA, 0)
+    iota(v("kio", A_ROWS[0], NSEG), [[16, NA]], 16 * A_ROWS[0], 0)
+    iota(v("n4"), [[0, C // 4], [1, 4]], 0, 0)
+    iota(v("n8"), [[0, K // 8], [1, 8]], 0, 0)
+    iota(v("jj"), [[4, C]], 0, 0)
+    fill(v("zt"), 0.0)
+    for j, (sh, msk) in enumerate([(0, 15), (4, 7), (2, 3), (0, 3), (1, 7), (0, 1)]):
+        ts(col("pi", j + 1), col("pi", 0), sh, A_.logical_shift_right, msk, A_.bitwise_and)
+    fill(v("a1", 3, C, 4), 0.0)
+    fill(v("a1", 4 * SHORT + 1, C, 4), 0.0)
+    fill(v("oo", C, C + K), 0.0)
+    copy(v("pc", 0, 6), v("pi", 1, 7))
+    p_r, p_g, p_r4, p_t, p_r2, p_h, p_nb, p_h2 = [col("pc", j) for j in range(8)]
+    pads = [(a, b) for s, lg, w, n in BLOCKS for a, b in ((w + row_words(s), w + SHORT), (w + SHORT + row_words(lg), w + n)) if b > a]
+    for a, b in pads[:-4]:
+        act(v("fl", 4 * a, 4 * b), v("zt", 0, 4 * (b - a)), F_.Copy)
+    for a, b in pads[-4:]:
+        fill(v("fl", 4 * a, 4 * b), 0.0)
+    ts(p_nb, p_r, -BIG, A_.mult)
+    ts(p_h2, p_h, 2.0, A_.add)
+    act(v("dabs"), v("dd"), F_.Abs, bias=-1.5)
+    for b in range(4):
+        ts(v("ct", 512 * b, 512 * b + 512), v("dd"), float(b), A_.is_equal)
+    ts(v("ct", 2048, 2560), v("dabs"), 2.0, A_.is_lt)
+    act(v("maska"), v("n16"), F_.Abs, bias=p_nb, scale=BIG)
+    act(v("cseg"), v("n16"), F_.Relu, bias=BIG, scale=-BIG)
+    act(v("keep16"), v("n16"), F_.Sign)
+    copy(v("uoff", 0, 8), v("ui"))
+    quant("qc", "sc", "ct", 0, 512)
+
+    for t in range(ROUNDS):
+        src = "x0" if t == 0 else "xs"
+        qy, sy = "qy%d" % t, "sy%d" % t
+
+        def evac(e, h, b):
+            out = v("ys", 4 * H * h + b, 4 * H * (h + 1), 4)
+            if e == "V":
+                ts(out, ps(4 * h + b, 0, H), 0.03125, A_.mult)
+            else:
+                act(out, ps(4 * h + b, 0, H), F_.Copy, scale=0.03125)
+
+        def layer(h):
+            for b in range(4):
+                mx(4 * h + b, "wq", "wp", 128 * b, "qx", "sx", H * h, H * h + H)
+        quant("qx", "sx", src, 0, H)
+        layer(0)
+        if t == 0:
+            for e, b in (("A", 0), ("V", 1), ("A", 2), ("V", 3)):
+                evac(e, 0, b)
+            quant("qx", "sx", src, H, C)
+            layer(1)
+            quant(qy, sy, "ys", 0, H)
+            quant("qu", "su", "ut", 0, 128)
+            evac("A", 1, 0)
+            evac("A", 1, 1)
+            op("V", lambda q: q.tensor_copy(T.qus[:, 0:128].bitcast(dt.uint32), T.qu[:, 0:128].bitcast(dt.uint32).indirect(T.uoff[:, 0:8])),
+               [v("qu"), v("uoff", 0, 8)], [v("qus")])
+            evac("V", 1, 2)
+            evac("A", 1, 3)
+            gather("A", v("sus"), v("su"), v("uoff", 0, 8))
+        else:
+            quant("qx", "sx", src, H, C)
+            layer(1)
+            for e, h, b in (("A", 0, 0), ("V", 0, 1), ("A", 0, 2), ("V", 0, 3), ("A", 1, 0), ("A", 1, 1)):
+                evac(e, h, b)
+            quant(qy, sy, "ys", 0, H)
+            evac("V", 1, 2)
+            evac("A", 1, 3)
+        quant(qy, sy, "ys", H, C)
+        mx(0, "qus", "sus", 0, qy, sy, 0, C)
+        mx(1, "qus", "sus", 0, qy, sy, 0, C)
+        pcs = pieces(t)
+        on = topo.engines(core, rel[0])
+        e4 = len(on) // 4
+
+        def send_codes(q, pcs=pcs, t=t):
+            tr = []
+            for i, p in enumerate(pcs[:4]):
+                rid, pid = topo.addr(rel[p[4]], core)
+                tr.append(RemoteDMATransfer(dst_ids=[DstId(rid=rid, pnc=pid)], dma_engine_mask=bits(on[e4 * i:e4 * i + e4]),
+                                            remote_sem=T.sem["ra%d" % t], src=side(T, p[0], p[2], p[3]), dst=side(T, p[1], p[2], p[3])))
+            q.remote_dma_fused(tr, local_sem=T.sem.left)
+
+        def send_scales(q, p=pcs[4], t=t):
+            rid, pid = topo.addr(rel[p[4]], core)
+            q.remote_dma(side(T, p[1], p[2], p[3]), side(T, p[0], p[2], p[3]), T.sem["ra%d" % t], T.sem.left, pid, rid, bits(on))
+        op("G", send_codes, [v(qy)], [], sem="")
+        op("G", send_scales, [v(sy)], [], sem="")
+        if t == 0:
+            ts(v("ct", 2560, 3072), v("cv"), p_g, A_.is_equal, -1.0, A_.mult)
+            act(v("a1", 7, C, 16), v("kio", 0, NSEG), F_.Identity, bias=p_r)
+            load("S", v("vt"), T.v[:], after=[v(qy)])
+        where, cut = {}, 16 * A_ROWS[0]
+        for b, (s, lg, w, n) in enumerate(BLOCKS):
+            where[s], where[lg] = (b, w), (b, w + SHORT)
+        last = [k for k in ORDER if k[0] == "c"][-1]
+        for k in ORDER:
+            if k[0] in "mh":
+                a, b = (cut, C) if k[1] == "a" else (0, cut)
+                if k[0] == "m":
+                    tt(v("mm", a, b), ps(0, a, b), v("maska", a, b), A_.add)
+                else:
+                    scan(v("hh", a, b), v("cseg", a, b), v("mm", a, b), A_.add, A_.min)
+                continue
+            if k[0] in "qcw":
+                s, lg, w, n = BLOCKS[k[1]]
+                if k[0] == "q":
+                    quant("qf", "sf", "fl", w, w + n)
+                elif k[0] == "c":
+                    mx(2, "qc", "sc", 640, "qf", "sf", w, w + n, k[1] == 0, k == last)
+                else:
+                    mx(3 + k[1] % 5, "qc", "sc", 512, "qf", "sf", w, w + n)
+                continue
+            m = k[1]
+            b, w = where[m]
+            row, own, acc = v("fl", 4 * w, 4 * (w + row_words(m))), col("hh", 16 * m + 15), col("a1", 16 * m + 3)
+            t0 = 16 * sum(a for a in A_ROWS if a < m)
+            if k[0] == "p":
+                act(v("tmp", t0, t0 + 16 * m), ps(1, 0, 16 * m), F_.Relu, bias=own, scale=-1.0)
+            elif k[0] == "r" and m in A_ROWS:
+                act(row, v("tmp", t0, t0 + 16 * m), F_.Sign, scale=-1.0, accum=acc)
+            elif k[0] == "r" and m == 0:
+                tt(row, ps(0, 0, C), v("hh"), A_.is_gt)
+                if t == 0:
+                    quant("qc", "sc", "ct", 512, 768)
+                    ts(v("mask4"), v("n4"), p_r4, A_.is_equal)
+            elif k[0] == "r":
+                ts(row, ps(0, 0, 16 * m), own, A_.is_ge)
+            elif 1 <= m <= NR:
+                add_up(acc, row)
+            elif BLOCKS[b][1] in A_ROWS:
+                act(v("junk", 112 * m, 112 * m + 16 * m), row, F_.Copy, accum=acc)
+            else:
+                part = ps(3 + b % 5, w - BLOCKS[b][2], w - BLOCKS[b][2] + row_words(m))
+                if m == 0:
+                    act(v("a1", 2, C, 4), part, F_.Copy)
+                else:
+                    act(v("junk", 112 * m, 112 * m + 4 * m), part, F_.Copy, accum=acc)
+        tt(v("a1", 0, C, 4), ps(2, SHORT, SHORT + C // 4), v("mask4", 0, C // 4), A_.mult)
+        tt(v("a1", 1, 4 * SHORT, 4), ps(2, 0, SHORT), v("mask4", 0, SHORT), A_.mult)
+        if t == 0:
+            act(v("keep8"), v("n8"), F_.Sign)
+            act(v("keep4"), v("n4"), F_.Sign)
+        scan(v("a2"), v("keep16"), v("a1"), A_.mult, A_.add)
+        if t == 0:
+            ts(v("mask8"), v("n8"), p_r2, A_.is_equal)
+        copy(v("offi", 0, NSEG), v("a2", 15, C, 16))
+        scatter(v("oo", 0, C), v("offi", 0, NSEG), v("jj"))
+        tt(v("l1", 0, K), v("oo", 0, K), v("mask8"), A_.mult)
+        tt(v("l1", K, 2 * K), v("oo", C - K, C), v("mask8"), A_.mult)
+        scan(v("l2", 0, K), v("keep8"), v("l1", 0, K), A_.mult, A_.add)
+        scan(v("l2", K, 2 * K), v("keep8"), v("l1", K, 2 * K), A_.mult, A_.add)
+        lo = v("lo%d" % t, 0, 4)
+        ts(lo, v("l2", 7, K, 8), 0.5, A_.mult, p_h, A_.add)
+
+        def send_list(q, t=t):
+            rid, pid = topo.addr(rel[0], core)
+            q.remote_dma(T["ll%d" % t][:, 0:4], T["lo%d" % t][:, 0:4], T.sem["rl%d" % t], T.sem.left, pid, rid, bits(on))
+        op("G", send_list, [lo], [], sem="")
+        nxt = (rank + 1) % len(T.cores)
+        noff = len(topo.engines(relays(T, topo, nxt)[0][0], core))
+        op("X", None, [], [v("lq%d" % t), v("lp%d" % t)], sem="ba%d" % t, val=4 * noff)
+        for b in range(4):
+            mx(4 + b, "qc", "sc", 128 * b, "lq%d" % t, "lp%d" % t, 0, C)
+        for b in range(4):
+            act(v("da" if b < 2 else "db", b % 2, 2 * C, 2), ps(4 + b, 0, C), F_.Copy)
+
+        def composed(a, b):
+            op("V", lambda q: q.tensor_tensor(ap(v("g1", a, b)), ap(v("oo", K, C + K)).indirect(ap(v("offi", a // 16, b // 16))),
+                                              ap(v("mask4", a, b)), A_.mult),
+               [v("oo", K, C + K), v("offi", a // 16, b // 16), v("mask4", a, b)], [v("g1", a, b)])
+        if t == ROUNDS - 1:
+            act(v("olb"), v("oo", 0, C), F_.Copy, scale=0.25)
+            for k in range(8):
+                store("S", T.ol[k:k + 1, :], T.olb[16 * k:16 * k + 1, :], [v("olb")])
+        composed(0, CA)
+        ts(v("offs", 0, 4), v("l2", K + 7, 2 * K, 8), p_h, A_.add)
+        scan(v("g2", 0, CA), v("keep4", 0, CA), v("g1", 0, CA), A_.mult, A_.add)
+        composed(CA, C)
+        ts(v("offx", 0, CA // 4), v("g2", 3, CA, 4), p_t, A_.add)
+        gather("A", v("xs", 0, 4 * CA), v("ys"), v("offx", 0, CA // 4))
+        scan(v("g2", CA, C), v("keep4", CA, C), v("g1", CA, C), A_.mult, A_.add)
+        ts(v("offs", 4, 8), v("l2", K + 7, 2 * K, 8), p_h2, A_.add)
+        ts(v("offx", CA // 4, C // 4), v("g2", CA + 3, C, 4), p_t, A_.add)
+        gather("V", v("xs", 4 * CA, 4 * C), v("ys"), v("offx", CA // 4, C // 4))
+        if t == 0:
+            quant("qv", "sv", "vt", 0, 128)
+        ll = v("ll%d" % t, 0, 4)
+        op("X", None, [], [ll], sem="la%d" % t, val=noff)
+        gather("V", v("gg", 0, 2 * K), v("da"), ll)
+        gather("A", v("gg", 2 * K, 4 * K), v("db"), ll)
+        scatter(v("xs"), v("offs", 0, 8), v("gg"))
+
+    for h in range(2):
+        quant("qx", "sx", "xs", H * h, H * h + H)
+    for h in range(2):
+        mx(h, "qv", "sv", 0, "qx", "sx", H * h, H * h + H)
+    store("S", T.oc[:, 0:4 * H], T.qx[:, 0:H].bitcast(dt.uint8), [v("qx", 0, H)])
+    act(v("yo", 0, H), ps(0, 0, H), F_.Copy)
+    copy(v("yo", H, C), ps(1, 0, H))
+    store("S", T.oc[:, 4 * H:4 * C], T.qx[:, H:C].bitcast(dt.uint8), [v("qx", H, C)])
+    store("A", T.y[:, 0:H], T.yo[:, 0:H], [v("yo", 0, H)])
+    for k in range(2):
+        store("S", T.osc[4 * k:4 * k + 4, :], T.sx[32 * k:32 * k + 4, :], [v("sx")])
+    store("S", T.y[:, H:C], T.yo[:, H:C], [v("yo", H, C)])
+    for k in range(2, 4):
+        store("A", T.osc[4 * k:4 * k + 4, :], T.sx[32 * k:32 * k + 4, :], [v("sx")])
+
+    needed = set()
+    for o in ops:
+        needed |= o["deps"]
+    count = {}
+    for i, o in enumerate(ops):
+        if o["sem"] is None and i in needed:
+            o["sem"] = "s" + o["e"]
+            count[o["sem"]] = o["val"] = count.get(o["sem"], 0) + 1
+            o["inc"] = 1
+        elif o["sem"] and o["fn"]:
+            o["inc"] = 16
+    seen = {e: {} for e in eng}
+    for o in ops:
+        if o["fn"] is None:
+            continue
+        want = {}
+        for d in o["deps"]:
+            s = ops[d]["sem"]
+            if s:
+                want[s] = max(want.get(s, 0), ops[d]["val"])
+        for s in sorted(want):
+            if seen[o["e"]].get(s, 0) < want[s]:
+                eng[o["e"]].wait_ge(T.sem[s], want[s])
+                seen[o["e"]][s] = want[s]
+        ins = o["fn"](eng[o["e"]])
+        if "inc" in o:
+            ins.then_inc(T.sem[o["sem"]], o["inc"])
+    g.sync.wait_ge(T.sem.st, 16 * stores[0])
+    g.wait_ge(T.sem.left, ROUNDS * 3 * len(topo.engines(core, rel[0])))

@@ -1,63 +1,81 @@
 from concourse.bass import DstId, RemoteDMATransfer
-from concourse.mybir import dt, AluOpType, ActivationFunctionType, AxisListType
+from concourse.mybir import dt, AluOpType, ActivationFunctionType
 
 C, K, ROUNDS = 448, 32, 3
-H = C // 2
 NSEG = C // 16
-NA = 7
-NR = 2
-SHORT = 56
-CA = 256
+M = 20
+E = 16 * M
+CUT3 = (0, 160, 320, 448)
+LOADS = "Sx0:320 Ap0:512 Aw0:256 Sw256:512 Ax320:448 Su0:128"
+LAYER0 = "x0 x1 m00 m01 m02 m03 E0 E1 A00 V01 A02 V03 m10 m11 m12 m13 x2 A10 y0 A11 V12 A13 u m20 m21 m22 m23 w A20 y1 A21 A22 V23 E2 E3 k"
+LAYER = "x0 x1 x2 m00 m01 m02 m03 A00 V01 A02 V03 m10 m11 m12 m13 A10 y0 A11 A12 V13 m20 m21 m22 m23 A20 y1 A21 A22 V23"
+ORDER = "y mb ma ha hb da p27 b v20 db p25 p26 qe g10 g14 g11 g12 qd f12 r27 r26 f11 g13 qw11 qr27 f14 p23 f16 p24 f15 r25 f13 p22 g15 r24 r23 qw13 f17 g16 g17 qw15 g18 f18 p21 qr25 qw17 f19 g19 r22 qr23 r21 s20 qw19 qz u e t"
+ROWS = "20 27 26 25 24 23 22 z 21"
+CUTS = "w11 w13 w15 w17 w19 r27 r25 r23 z"
+MOVE = "l1 l2 bt l3 c0:192 s0:192 c192:320 o0:192 s192:320 c320:480 gA0:192 o192:320 s320:480 gV192:320 o320:480"
+LATEG = "A0:128"
+LAST = "x0 x1 x2 m0 m1 m2 c0S3 s0S s1S s2S s3S A0 V1 V2 y0A3"
 BIG = 2.0 ** 90
-CODE = "float8_e4m3fn_x4"
+CODE, F16 = "float8_e4m3fn_x4", "float16"
+PRE = 128 - 4 * M
+A_ROWS = list(range(NSEG - 1, M - 1, -1))
+DS = list(range(M // 2, M))
 
 
-def row_words(m):
-    return 4 * m if m else C // 4
+def layout():
+    first = PRE + C // 4
+    win = {d: first + 4 * (M + 1) * i for i, d in enumerate(DS)}
+    end = first + 4 * (M + 1) * len(DS)
+    zero = [(0, PRE), (first, first + 2 * M), (end, end + PRE)] + [(w + 4 * M, w + 4 * M + 4) for w in win.values()]
+    row, w, z = {}, end + PRE, {}
+    for m in ROWS.split():
+        if m[0] == "z":
+            zero.append((w, w + PRE))
+            z[m], w = w, w + PRE
+        else:
+            row[int(m)] = w
+            w += 4 * int(m)
+    chunk, a, name = {}, 0, "d"
+    for c in CUTS.split() + ["end"]:
+        b = z[c] if c in z else w if c == "end" else (win if c[0] == "w" else row)[int(c[1:])]
+        if a < end < b:
+            chunk[name] = (a, max(end, a + 128))
+            a, name = end, "e"
+        chunk[name] = (a, b)
+        a, name = b, c
+    return win, end, zero, row, w, chunk
 
 
-def blocks():
-    longs = [0] + list(range(NSEG - 1 - NA, NSEG // 2, -1)) + list(range(NSEG - 1, NSEG - 1 - NA, -1))
-    out, w = [], 0
-    for i, lg in enumerate(longs):
-        n = SHORT + max(row_words(lg), 128 - SHORT)
-        out.append((NSEG // 2 - i, lg, w, n))
-        w += n
-    return out, w
-
-
-BLOCKS, NW = blocks()
-A_ROWS = list(range(NSEG - NA, NSEG))
-ORDER = [(x[0], x[1:]) if x[0] in "mh" else (x[0], int(x[1:])) for x in (
-    "ma ha mb p23 hb p22 r0 r17 r7 r10 r20 r14 r23 p21 r9 r18 r19 q0 r4 w0 p25 p24 r21 p27 r11 p26 c0 r22 r12 r13 r26 q4 q2 w4 r27 s0 q1 w1 q3 "
-    "s14 w3 c3 r25 r16 r24 s13 r15 c2 w2 c4 s20 q7 c7 r8 r3 r1 s18 c1 q5 r6 w5 s6 s7 q6 s17 s11 c5 r5 s3 w6 r2 q8 q9 c6 s10 q10 s8 s5 q11 c8 c9 "
-    "q12 q13 c10 s19 s2 c11 s12 c12 c13 s15 s9 s4 s16 s1").split()]
+WIN, END, ZERO, ROW, NW, CHUNK = layout()
 
 SCRATCH = {
-    "x0": ("sbuf", [128, 4 * C], "bfloat16"), "xs": ("sbuf", [128, 4 * C], "bfloat16"), "ys": ("sbuf", [128, 4 * C], "bfloat16"),
-    "qx": ("sbuf", [128, C], CODE), "sx": ("sbuf", [128, C], "uint8"),
+    "x0": ("sbuf", [128, 4 * C], "bfloat16"), "xs": ("sbuf", [128, 4 * C], "bfloat16"), "xl": ("sbuf", [128, 4 * C], "bfloat16"),
+    "ys": ("sbuf", [128, 4 * (C + K)], "bfloat16"), "qx": ("sbuf", [128, C], CODE), "sx": ("sbuf", [128, C], "uint8"),
     "wq": ("sbuf", [128, 512], CODE), "wp": ("sbuf", [128, 512], "uint8"),
     "ut": ("sbuf", [128, 512], "bfloat16"), "qu": ("sbuf", [128, 128], CODE), "su": ("sbuf", [128, 128], "uint8"),
     "qus": ("sbuf", [128, 128], CODE), "sus": ("sbuf", [128, 128], "uint8"),
     "vt": ("sbuf", [128, 512], "bfloat16"), "qv": ("sbuf", [128, 128], CODE), "sv": ("sbuf", [128, 128], "uint8"),
-    "mm": ("sbuf", [128, C], "float32"), "hh": ("sbuf", [128, C], "float32"),
+    "mm": ("sbuf", [128, C], "float32"), "hh": ("sbuf", [128, C], "float32"), "hb": ("sbuf", [128, E], "float32"),
     "fl": ("sbuf", [128, 4 * NW], "bfloat16"), "qf": ("sbuf", [128, NW], CODE), "sf": ("sbuf", [128, NW], "uint8"),
-    "tmp": ("sbuf", [128, 16 * sum(A_ROWS)], "bfloat16"), "junk": ("sbuf", [128, (NSEG - NA) * 112], "bfloat16"),
-    "a1": ("sbuf", [128, C], "float32"), "a2": ("sbuf", [128, C], "float32"),
+    "tmp": ("sbuf", [128, 16 * sum(A_ROWS)], "bfloat16"), "acc": ("sbuf", [128, 16], "float32"),
+    "a1": ("sbuf", [128, 12 * NSEG], F16), "a2": ("sbuf", [128, 12 * NSEG], F16),
     "offi": ("sbuf", [128, 32], "uint16"), "oo": ("sbuf", [128, C + K], "float32"),
-    "g1": ("sbuf", [128, C], "float32"), "g2": ("sbuf", [128, C], "float32"), "offx": ("sbuf", [128, C // 4], "uint16"),
-    "l1": ("sbuf", [128, 2 * K], "float32"), "l2": ("sbuf", [128, 2 * K], "float32"), "offs": ("sbuf", [128, 16], "uint16"),
-    "da": ("sbuf", [128, 2 * C], "bfloat16"), "db": ("sbuf", [128, 2 * C], "bfloat16"), "gg": ("sbuf", [128, 4 * K], "bfloat16"),
+    "g1": ("sbuf", [128, C + K], F16), "g2": ("sbuf", [128, C + K], F16), "offx": ("sbuf", [128, 128], "uint16"),
+    "l1": ("sbuf", [128, K], F16), "l2": ("sbuf", [128, K], F16),
+    "da": ("sbuf", [128, 2 * C], "bfloat16"), "db": ("sbuf", [128, 2 * C], "bfloat16"),
     "yo": ("sbuf", [128, C], "float32"), "olb": ("sbuf", [128, C], "float32"),
     "pi": ("sbuf", [128, 8], "int32"), "pc": ("sbuf", [128, 16], "float32"),
     "ui": ("sbuf", [128, 8], "int32"), "uoff": ("sbuf", [128, 16], "uint16"),
-    "dd": ("sbuf", [128, 512], "bfloat16"), "dabs": ("sbuf", [128, 512], "bfloat16"), "cv": ("sbuf", [128, 512], "bfloat16"),
-    "ct": ("sbuf", [128, 6 * 512], "bfloat16"), "qc": ("sbuf", [128, 6 * 128], CODE), "sc": ("sbuf", [128, 6 * 128], "uint8"),
-    "n16": ("sbuf", [128, C], "bfloat16"), "n4": ("sbuf", [128, C], "bfloat16"), "n8": ("sbuf", [128, K], "bfloat16"),
-    "maska": ("sbuf", [128, C], "bfloat16"), "cseg": ("sbuf", [128, C], "bfloat16"), "keep16": ("sbuf", [128, C], "bfloat16"),
-    "keep4": ("sbuf", [128, C], "bfloat16"), "mask4": ("sbuf", [128, C], "bfloat16"),
+    "hi": ("sbuf", [128, 32], "int32"), "hoff": ("sbuf", [128, 32], "uint16"),
+    "dd": ("sbuf", [128, 516], "bfloat16"), "ce": ("sbuf", [128, 516], "bfloat16"), "dabs": ("sbuf", [128, 512], "bfloat16"),
+    "cv": ("sbuf", [128, 32], "bfloat16"), "ct": ("sbuf", [128, 1024], "bfloat16"),
+    "qc": ("sbuf", [128, 6 * 128], CODE), "sc": ("sbuf", [128, 6 * 128], "uint8"),
+    "n16": ("sbuf", [128, C], "bfloat16"), "n4": ("sbuf", [128, C + K], "bfloat16"), "n8": ("sbuf", [128, K], "bfloat16"),
+    "n12": ("sbuf", [128, 12 * NSEG], "bfloat16"), "keep12": ("sbuf", [128, 12 * NSEG], "bfloat16"),
+    "maska": ("sbuf", [128, C], "bfloat16"), "cseg": ("sbuf", [128, C], "bfloat16"),
+    "keep4": ("sbuf", [128, C + K], "bfloat16"), "mask4": ("sbuf", [128, C + K], "bfloat16"),
     "keep8": ("sbuf", [128, K], "bfloat16"), "mask8": ("sbuf", [128, K], "bfloat16"),
-    "jj": ("sbuf", [128, C], "float32"), "kio": ("sbuf", [128, 32], "float32"), "zt": ("sbuf", [128, 4 * SHORT], "bfloat16"),
+    "jj": ("sbuf", [128, C], "float32"), "kio": ("sbuf", [128, 32], "float32"), "zt": ("sbuf", [128, 256], "bfloat16"),
 }
 for _t in range(ROUNDS):
     SCRATCH["qy%d" % _t] = ("sbuf", [128, C], CODE)
@@ -69,7 +87,7 @@ for _t in range(ROUNDS):
 for _b in range(8):
     SCRATCH["ps%d" % _b] = ("psum", [128, 512], "float32")
 
-SEMAPHORES = (["sV", "sA", "sP", "sG", "st", "left"] + ["ld%d" % i for i in range(7)]
+SEMAPHORES = (["sV", "sA", "sP", "sG", "st", "left"] + ["ld%d" % i for i in range(9)]
               + ["%s%d" % (s, t) for s in ("ra", "rl", "ba", "la") for t in range(ROUNDS)])
 
 A_, F_ = AluOpType, ActivationFunctionType
@@ -173,9 +191,6 @@ def rank_program(g, core, T, topo):
     def fill(out, c):
         op("V", lambda q: q.memset(ap(out), c), [], [out])
 
-    def add_up(out, in_):
-        op("V", lambda q: q.tensor_reduce(ap(out), ap(in_), AxisListType.X, A_.add), [in_], [out])
-
     def act(out, in_, f, bias=None, scale=None, accum=None):
         kw = {}
         if bias is not None:
@@ -196,9 +211,9 @@ def rank_program(g, core, T, topo):
     def scatter(win, off, in_):
         op("V", lambda q: q.tensor_copy(ap(win).indirect(ap(off)), ap(in_)), [in_, off], [win])
 
-    def quant(q, s, src, a, b):
-        op("V", lambda e: e.quantize_mx(ap(v(q, a, b)), ap(v(s, a, b)), ap(v(src, 4 * a, 4 * b))),
-           [v(src, 4 * a, 4 * b)], [v(q, a, b), v(s, a, b)])
+    def quant(q, s, src, a, b, at=None):
+        i = v(src, 4 * a, 4 * b) if at is None else v(src, at, at + 4 * (b - a))
+        op("V", lambda e: e.quantize_mx(ap(v(q, a, b)), ap(v(s, a, b)), ap(i)), [i], [v(q, a, b), v(s, a, b)])
 
     def mx(bank, lq, ls, la, rq, rs, a, b, start=True, stop=True):
         out = v("ps%d" % bank, 0, b - a)
@@ -228,90 +243,76 @@ def rank_program(g, core, T, topo):
     def col(name, j):
         return v(name, j, j + 1)
 
-    load("S", v("x0", 0, 4 * H), T.x[:, 0:4 * H])
-    load("A", v("wp"), T.ws[:])
-    load("A", v("wq", 0, 256), T.wc[:, 0:1024])
-    load("S", v("wq", 256, 512), T.wc[:, 1024:2048])
-    load("S", v("x0", 4 * H, 4 * C), T.x[:, 4 * H:4 * C])
-    load("A", v("ut"), T.u[:])
+    for k in LOADS.split():
+        a, b = [int(i) for i in k[2:].split(":")]
+        name, whole, n = {"x": ("x0", T.x, 4), "w": ("wq", T.wc, 4), "p": ("wp", T.ws, 1), "u": ("ut", T.u, 4)}[k[1]]
+        load(k[0], v(name, a, b) if k[1] in "wp" else v(name, 4 * a, 4 * b), whole[:, n * a:n * b])
 
     iota(col("pi", 0), [[0, 1]], 0, 1)
-    iota(v("dd"), [[1, 512]], 0, -4)
+    iota(v("dd"), [[1, 516]], -3, -4)
+    iota(v("cv"), [[1, 8], [0, 4]], 0, 0)
     iota(v("n16"), [[0, NSEG], [1, 16]], 0, 0)
     iota(v("ui"), [[16, 8]], 0, 0)
-    for t in range(4):
-        iota(v("cv", t, 512, 4), [[1, 8], [0, 4], [-8, 4]], 8 * t, 0)
-    iota(v("kio", 0, A_ROWS[0]), [[-16, A_ROWS[0]]], C - 16 - 16 * NA, 0)
-    iota(v("kio", A_ROWS[0], NSEG), [[16, NA]], 16 * A_ROWS[0], 0)
-    iota(v("n4"), [[0, C // 4], [1, 4]], 0, 0)
+    iota(v("hi", 0, M), [[16, M]], 15, 0)
+    iota(v("kio", 0, M), [[16, 2], [0, M // 2]], 16 * len(DS) - 16, 0)
+    iota(v("kio", M, NSEG), [[16, NSEG - M]], 16 * M, 0)
+    iota(v("n4"), [[0, (C + K) // 4], [1, 4]], 0, 0)
     iota(v("n8"), [[0, K // 8], [1, 8]], 0, 0)
-    iota(v("jj"), [[4, C]], 0, 0)
     fill(v("zt"), 0.0)
     for j, (sh, msk) in enumerate([(0, 15), (4, 7), (2, 3), (0, 3), (1, 7), (0, 1)]):
         ts(col("pi", j + 1), col("pi", 0), sh, A_.logical_shift_right, msk, A_.bitwise_and)
-    fill(v("a1", 3, C, 4), 0.0)
-    fill(v("a1", 4 * SHORT + 1, C, 4), 0.0)
-    fill(v("oo", C, C + K), 0.0)
+    fill(v("ct", 512, 1024), 0.0)
     copy(v("pc", 0, 6), v("pi", 1, 7))
-    p_r, p_g, p_r4, p_t, p_r2, p_h, p_nb, p_h2 = [col("pc", j) for j in range(8)]
-    pads = [(a, b) for s, lg, w, n in BLOCKS for a, b in ((w + row_words(s), w + SHORT), (w + SHORT + row_words(lg), w + n)) if b > a]
-    for a, b in pads[:-4]:
+    copy(v("a1", 2, 12 * NSEG, 3), v("zt", 0, 4 * NSEG))
+    fill(v("ys", 4 * C, 4 * (C + K)), 0.0)
+    p_r, p_g, p_r4, p_t, p_r2, p_h, p_nb = [col("pc", j) for j in range(7)]
+    for a, b in ZERO:
         act(v("fl", 4 * a, 4 * b), v("zt", 0, 4 * (b - a)), F_.Copy)
-    for a, b in pads[-4:]:
-        fill(v("fl", 4 * a, 4 * b), 0.0)
     ts(p_nb, p_r, -BIG, A_.mult)
-    ts(p_h2, p_h, 2.0, A_.add)
-    act(v("dabs"), v("dd"), F_.Abs, bias=-1.5)
-    for b in range(4):
-        ts(v("ct", 512 * b, 512 * b + 512), v("dd"), float(b), A_.is_equal)
-    ts(v("ct", 2048, 2560), v("dabs"), 2.0, A_.is_lt)
+    act(v("dabs"), v("dd", 3, 515), F_.Abs, bias=-1.5)
+    ts(v("ce"), v("dd"), 0.0, A_.is_equal)
+    for t in range(4):
+        ts(v("ct", 512 + 5 * t, 1024, 16), v("cv"), p_g, A_.is_equal, -1.0, A_.mult)
+    ts(v("ct", 0, 512), v("dabs"), 2.0, A_.is_lt)
     act(v("maska"), v("n16"), F_.Abs, bias=p_nb, scale=BIG)
     act(v("cseg"), v("n16"), F_.Relu, bias=BIG, scale=-BIG)
-    act(v("keep16"), v("n16"), F_.Sign)
+    quant("qc", "sc", "ct", 512, 768, 0)
     copy(v("uoff", 0, 8), v("ui"))
-    quant("qc", "sc", "ct", 0, 512)
+    copy(v("hoff", 0, M), v("hi", 0, M))
+    src = ("x0", "x0")
 
     for t in range(ROUNDS):
-        src = "x0" if t == 0 else "xs"
         qy, sy = "qy%d" % t, "sy%d" % t
-
-        def evac(e, h, b):
-            out = v("ys", 4 * H * h + b, 4 * H * (h + 1), 4)
-            if e == "V":
-                ts(out, ps(4 * h + b, 0, H), 0.03125, A_.mult)
+        for k in (LAYER if t else LAYER0).split():
+            if k == "u":
+                quant("qu", "su", "ut", 0, 128)
+            elif k == "w":
+                op("V", lambda q: q.tensor_copy(T.qus[:, 0:128].bitcast(dt.uint32), T.qu[:, 0:128].bitcast(dt.uint32).indirect(T.uoff[:, 0:8])),
+                   [v("qu"), v("uoff", 0, 8)], [v("qus")])
+                gather("A", v("sus"), v("su"), v("uoff", 0, 8))
+            elif k == "k":
+                ts(v("mask4"), v("n4"), p_r4, A_.is_equal)
+                ts(v("a1", 2, 12 * NSEG, 12), v("kio", 0, NSEG), p_r, A_.add)
+            elif k[0] == "E":
+                b = int(k[1])
+                quant("qc", "sc", "ce", 128 * b, 128 * b + 128, 3 - b)
             else:
-                act(out, ps(4 * h + b, 0, H), F_.Copy, scale=0.03125)
-
-        def layer(h):
-            for b in range(4):
-                mx(4 * h + b, "wq", "wp", 128 * b, "qx", "sx", H * h, H * h + H)
-        quant("qx", "sx", src, 0, H)
-        layer(0)
-        if t == 0:
-            for e, b in (("A", 0), ("V", 1), ("A", 2), ("V", 3)):
-                evac(e, 0, b)
-            quant("qx", "sx", src, H, C)
-            layer(1)
-            quant(qy, sy, "ys", 0, H)
-            quant("qu", "su", "ut", 0, 128)
-            evac("A", 1, 0)
-            evac("A", 1, 1)
-            op("V", lambda q: q.tensor_copy(T.qus[:, 0:128].bitcast(dt.uint32), T.qu[:, 0:128].bitcast(dt.uint32).indirect(T.uoff[:, 0:8])),
-               [v("qu"), v("uoff", 0, 8)], [v("qus")])
-            evac("V", 1, 2)
-            evac("A", 1, 3)
-            gather("A", v("sus"), v("su"), v("uoff", 0, 8))
-        else:
-            quant("qx", "sx", src, H, C)
-            layer(1)
-            for e, h, b in (("A", 0, 0), ("V", 0, 1), ("A", 0, 2), ("V", 0, 3), ("A", 1, 0), ("A", 1, 1)):
-                evac(e, h, b)
-            quant(qy, sy, "ys", 0, H)
-            evac("V", 1, 2)
-            evac("A", 1, 3)
-        quant(qy, sy, "ys", H, C)
-        mx(0, "qus", "sus", 0, qy, sy, 0, C)
-        mx(1, "qus", "sus", 0, qy, sy, 0, C)
+                h = int(k[1])
+                a, z = CUT3[h], CUT3[h + 1]
+                if k[0] == "x":
+                    quant("qx", "sx", src[h // 2], a, z)
+                elif k[0] == "y":
+                    quant(qy, sy, "ys", a, z)
+                else:
+                    b = int(k[2])
+                    bank, out = b + 4 * (1 - h % 2), v("ys", 4 * a + b, 4 * z, 4)
+                    if k[0] == "m":
+                        mx(bank, "wq", "wp", 128 * b, "qx", "sx", a, z)
+                    elif k[0] == "V":
+                        ts(out, ps(bank, 0, z - a), 0.03125, A_.mult)
+                    else:
+                        act(out, ps(bank, 0, z - a), F_.Copy, scale=0.03125)
+        mx(0, "qus", "sus", 0, qy, sy, 0, E)
         pcs = pieces(t)
         on = topo.engines(core, rel[0])
         e4 = len(on) // 4
@@ -327,127 +328,146 @@ def rank_program(g, core, T, topo):
         def send_scales(q, p=pcs[4], t=t):
             rid, pid = topo.addr(rel[p[4]], core)
             q.remote_dma(side(T, p[1], p[2], p[3]), side(T, p[0], p[2], p[3]), T.sem["ra%d" % t], T.sem.left, pid, rid, bits(on))
-        op("G", send_codes, [v(qy)], [], sem="")
-        op("G", send_scales, [v(sy)], [], sem="")
-        if t == 0:
-            ts(v("ct", 2560, 3072), v("cv"), p_g, A_.is_equal, -1.0, A_.mult)
-            act(v("a1", 7, C, 16), v("kio", 0, NSEG), F_.Identity, bias=p_r)
-            load("S", v("vt"), T.v[:], after=[v(qy)])
-        where, cut = {}, 16 * A_ROWS[0]
-        for b, (s, lg, w, n) in enumerate(BLOCKS):
-            where[s], where[lg] = (b, w), (b, w + SHORT)
-        last = [k for k in ORDER if k[0] == "c"][-1]
-        for k in ORDER:
-            if k[0] in "mh":
-                a, b = (cut, C) if k[1] == "a" else (0, cut)
-                if k[0] == "m":
-                    tt(v("mm", a, b), ps(0, a, b), v("maska", a, b), A_.add)
-                else:
-                    scan(v("hh", a, b), v("cseg", a, b), v("mm", a, b), A_.add, A_.min)
-                continue
-            if k[0] in "qcw":
-                s, lg, w, n = BLOCKS[k[1]]
-                if k[0] == "q":
-                    quant("qf", "sf", "fl", w, w + n)
-                elif k[0] == "c":
-                    mx(2, "qc", "sc", 640, "qf", "sf", w, w + n, k[1] == 0, k == last)
-                else:
-                    mx(3 + k[1] % 5, "qc", "sc", 512, "qf", "sf", w, w + n)
-                continue
-            m = k[1]
-            b, w = where[m]
-            row, own, acc = v("fl", 4 * w, 4 * (w + row_words(m))), col("hh", 16 * m + 15), col("a1", 16 * m + 3)
-            t0 = 16 * sum(a for a in A_ROWS if a < m)
-            if k[0] == "p":
-                act(v("tmp", t0, t0 + 16 * m), ps(1, 0, 16 * m), F_.Relu, bias=own, scale=-1.0)
-            elif k[0] == "r" and m in A_ROWS:
-                act(row, v("tmp", t0, t0 + 16 * m), F_.Sign, scale=-1.0, accum=acc)
-            elif k[0] == "r" and m == 0:
-                tt(row, ps(0, 0, C), v("hh"), A_.is_gt)
+
+        t0 = {m: 16 * sum(a for a in A_ROWS if a > m) for m in A_ROWS}
+        sums = [("c", PRE, C // 4), ("w", PRE, C // 4)] + [("c", WIN[d], 4 * M) for d in DS] + [("c", ROW[m], 4 * m) for m in A_ROWS]
+        sums += [("w", END - 4 * M * i, 4 * M) for i in range(1, len(DS) + 1)]
+        have, begun = set(), set()
+        for k in ORDER.split():
+            m = int(k[1:]) if k[1:].isdigit() else 0
+            a, b = (E, C) if k[1:] == "a" else (0, E)
+            score = ps(5, 0, C - E) if a else ps(0, 0, E)
+            if k == "y":
+                quant(qy, sy, "ys", E, C)
+                mx(5, "qus", "sus", 0, qy, sy, E, C)
+                mx(1, "qus", "sus", 0, qy, sy, 0, C)
+                op("G", send_codes, [v(qy)], [], sem="")
+                op("G", send_scales, [v(sy)], [], sem="")
                 if t == 0:
-                    quant("qc", "sc", "ct", 512, 768)
-                    ts(v("mask4"), v("n4"), p_r4, A_.is_equal)
-            elif k[0] == "r":
-                ts(row, ps(0, 0, 16 * m), own, A_.is_ge)
-            elif 1 <= m <= NR:
-                add_up(acc, row)
-            elif BLOCKS[b][1] in A_ROWS:
-                act(v("junk", 112 * m, 112 * m + 16 * m), row, F_.Copy, accum=acc)
-            else:
-                part = ps(3 + b % 5, w - BLOCKS[b][2], w - BLOCKS[b][2] + row_words(m))
-                if m == 0:
-                    act(v("a1", 2, C, 4), part, F_.Copy)
+                    act(v("keep8"), v("n8"), F_.Sign)
+                    act(v("keep4"), v("n4"), F_.Sign)
+                    iota(v("n12"), [[0, NSEG], [1, 12]], 0, 0)
+                    iota(v("jj"), [[4, C]], 0, 0)
+                    iota(v("oo", C, C + K), [[4, K]], 4 * C, 0)
+            elif k[0] == "m":
+                tt(v("mm", a, b), score, v("maska", a, b), A_.add)
+            elif k[0] == "h":
+                scan(v("hh", a, b), v("cseg", a, b), v("mm", a, b), A_.add, A_.min)
+            elif k == "b":
+                gather("A", v("hb"), v("hh", 0, E), v("hoff", 0, M))
+            elif k[0] == "d":
+                tt(v("fl", 4 * PRE + a, 4 * PRE + b), score, v("hh", a, b), A_.is_gt)
+            elif k[0] in "fg":
+                w, n = 4 * WIN[m], 16 * (M - m)
+                if k[0] == "f":
+                    tt(v("fl", w, w + n), ps(0, 0, n), v("hb", E - n, E), A_.is_ge)
                 else:
-                    act(v("junk", 112 * m, 112 * m + 4 * m), part, F_.Copy, accum=acc)
-        tt(v("a1", 0, C, 4), ps(2, SHORT, SHORT + C // 4), v("mask4", 0, C // 4), A_.mult)
-        tt(v("a1", 1, 4 * SHORT, 4), ps(2, 0, SHORT), v("mask4", 0, SHORT), A_.mult)
-        if t == 0:
-            act(v("keep8"), v("n8"), F_.Sign)
-            act(v("keep4"), v("n4"), F_.Sign)
-        scan(v("a2"), v("keep16"), v("a1"), A_.mult, A_.add)
+                    tt(v("fl", w + n, w + E), ps(0, n, E), v("hb", 0, E - n), A_.is_gt)
+            elif k[0] in "vspr":
+                row, mid, own = v("fl", 4 * ROW[m], 4 * ROW[m] + 16 * m), v("tmp", t0[m], t0[m] + 16 * m), col("hh", 16 * m + 15)
+                if k[0] == "v":
+                    ts(row, ps(0, 0, 16 * m), own, A_.is_lt, -1.0, A_.mult)
+                elif k[0] == "s":
+                    act(mid, row, F_.Copy, accum=col("acc", m - M))
+                elif k[0] == "p":
+                    act(mid, ps(1, 0, 16 * m), F_.Relu, bias=own, scale=-1.0)
+                else:
+                    act(row, mid, F_.Sign, scale=-1.0, accum=col("acc", m - M))
+            elif k == "u":
+                copy(v("a1", 12 * M + 5, 12 * NSEG, 12), v("acc", 0, NSEG - M))
+            elif k == "e":
+                copy(v("a1", 1, 12 * NSEG, 3), ps(3, PRE, PRE + C // 4))
+            elif k == "t":
+                if t == 0:
+                    ts(v("keep12"), v("n12"), 0.5, A_.is_gt)
+                tt(v("a1", 0, 12 * NSEG, 3), ps(2, PRE, PRE + C // 4), v("mask4", 0, C // 4), A_.mult)
+            else:
+                quant("qf", "sf", "fl", *CHUNK[k[1:]])
+                have |= set(range(*CHUNK[k[1:]]))
+                for x in sorted(sums, key=lambda x: (x[0] == "c", x[1])):
+                    if all(w in have for w in range(x[1] - PRE, x[1] + x[2])) and (x[0] in begun or x[1] == PRE):
+                        sums.remove(x)
+                        c = x[0] == "c"
+                        mx(2 if c else 3, "qc", "sc", 640 if c else 512, "qf", "sf", x[1] - PRE, x[1] + x[2],
+                           x[0] not in begun, all(y[0] != x[0] for y in sums))
+                        begun.add(x[0])
+        scan(v("a2"), v("keep12"), v("a1"), A_.mult, A_.add)
         if t == 0:
             ts(v("mask8"), v("n8"), p_r2, A_.is_equal)
-        copy(v("offi", 0, NSEG), v("a2", 15, C, 16))
+        copy(v("offi", 0, NSEG), v("a2", 11, 12 * NSEG, 12))
         scatter(v("oo", 0, C), v("offi", 0, NSEG), v("jj"))
-        tt(v("l1", 0, K), v("oo", 0, K), v("mask8"), A_.mult)
-        tt(v("l1", K, 2 * K), v("oo", C - K, C), v("mask8"), A_.mult)
-        scan(v("l2", 0, K), v("keep8"), v("l1", 0, K), A_.mult, A_.add)
-        scan(v("l2", K, 2 * K), v("keep8"), v("l1", K, 2 * K), A_.mult, A_.add)
-        lo = v("lo%d" % t, 0, 4)
-        ts(lo, v("l2", 7, K, 8), 0.5, A_.mult, p_h, A_.add)
-
-        def send_list(q, t=t):
-            rid, pid = topo.addr(rel[0], core)
-            q.remote_dma(T["ll%d" % t][:, 0:4], T["lo%d" % t][:, 0:4], T.sem["rl%d" % t], T.sem.left, pid, rid, bits(on))
-        op("G", send_list, [lo], [], sem="")
         nxt = (rank + 1) % len(T.cores)
         noff = len(topo.engines(relays(T, topo, nxt)[0][0], core))
         op("X", None, [], [v("lq%d" % t), v("lp%d" % t)], sem="ba%d" % t, val=4 * noff)
         for b in range(4):
             mx(4 + b, "qc", "sc", 128 * b, "lq%d" % t, "lp%d" % t, 0, C)
+        if t == 1:
+            load("S", v("vt"), T.v[:], after=[v("lq1")])
         for b in range(4):
-            act(v("da" if b < 2 else "db", b % 2, 2 * C, 2), ps(4 + b, 0, C), F_.Copy)
+            act(v("db" if b % 2 else "da", b // 2, 2 * C, 2), ps(4 + b, 0, C), F_.Copy)
+        if t == ROUNDS - 1:
+            act(v("olb"), v("oo", 0, C), F_.Copy, scale=0.25)
+            for k in range(8):
+                store("S", T.ol[k:k + 1, :], T.olb[16 * k:16 * k + 1, :], [v("olb")])
+        lo = v("lo%d" % t, 0, 4)
+
+        def send_list(q, t=t):
+            rid, pid = topo.addr(rel[0], core)
+            q.remote_dma(T["ll%d" % t][:, 0:4], T["lo%d" % t][:, 0:4], T.sem["rl%d" % t], T.sem.left, pid, rid, bits(on))
 
         def composed(a, b):
             op("V", lambda q: q.tensor_tensor(ap(v("g1", a, b)), ap(v("oo", K, C + K)).indirect(ap(v("offi", a // 16, b // 16))),
                                               ap(v("mask4", a, b)), A_.mult),
                [v("oo", K, C + K), v("offi", a // 16, b // 16), v("mask4", a, b)], [v("g1", a, b)])
+        for k in MOVE.split():
+            if k == "l1":
+                tt(v("l1"), v("oo", 0, K), v("mask8"), A_.mult)
+            elif k == "l2":
+                scan(v("l2"), v("keep8"), v("l1"), A_.mult, A_.add)
+            elif k == "l3":
+                ts(lo, v("l2", 7, K, 8), 0.5, A_.mult, p_h, A_.add)
+                op("G", send_list, [lo], [], sem="")
+            elif k == "bt":
+                tt(v("g1", C, C + K), v("oo", C - K, C), v("mask4", 0, K), A_.mult)
+            else:
+                a, b = [int(x) for x in k.lstrip("csogAV").split(":")]
+                if k[0] == "c":
+                    composed(a, min(b, C))
+                elif k[0] == "s":
+                    scan(v("g2", a, b), v("keep4", a, b), v("g1", a, b), A_.mult, A_.add)
+                elif k[0] == "o":
+                    ts(v("offx", a // 4, b // 4), v("g2", a + 3, b, 4), p_t, A_.add)
+                else:
+                    gather(k[1], v("xs", 4 * a, 4 * b), v("ys"), v("offx", a // 4, b // 4))
         if t == ROUNDS - 1:
-            act(v("olb"), v("oo", 0, C), F_.Copy, scale=0.25)
-            for k in range(8):
-                store("S", T.ol[k:k + 1, :], T.olb[16 * k:16 * k + 1, :], [v("olb")])
-        composed(0, CA)
-        ts(v("offs", 0, 4), v("l2", K + 7, 2 * K, 8), p_h, A_.add)
-        scan(v("g2", 0, CA), v("keep4", 0, CA), v("g1", 0, CA), A_.mult, A_.add)
-        composed(CA, C)
-        ts(v("offx", 0, CA // 4), v("g2", 3, CA, 4), p_t, A_.add)
-        gather("A", v("xs", 0, 4 * CA), v("ys"), v("offx", 0, CA // 4))
-        scan(v("g2", CA, C), v("keep4", CA, C), v("g1", CA, C), A_.mult, A_.add)
-        ts(v("offs", 4, 8), v("l2", K + 7, 2 * K, 8), p_h2, A_.add)
-        ts(v("offx", CA // 4, C // 4), v("g2", CA + 3, C, 4), p_t, A_.add)
-        gather("V", v("xs", 4 * CA, 4 * C), v("ys"), v("offx", CA // 4, C // 4))
-        if t == 0:
             quant("qv", "sv", "vt", 0, 128)
         ll = v("ll%d" % t, 0, 4)
         op("X", None, [], [ll], sem="la%d" % t, val=noff)
-        gather("V", v("gg", 0, 2 * K), v("da"), ll)
-        gather("A", v("gg", 2 * K, 4 * K), v("db"), ll)
-        scatter(v("xs"), v("offs", 0, 8), v("gg"))
+        gather("V", v("ys", 4 * C, 4 * (C + K), 2), v("da"), ll)
+        gather("A", v("ys", 4 * C + 1, 4 * (C + K), 2), v("db"), ll)
+        scatter(v("xs"), v("offx", C // 4, (C + K) // 4), v("ys", 4 * C, 4 * (C + K)))
+        for k in LATEG.split():
+            a, b = [E + int(x) for x in k[1:].split(":")]
+            gather(k[0], v("xl", 4 * a, 4 * b), v("ys"), v("offx", a // 4, b // 4))
+        src = ("xs", "xl")
 
-    for h in range(2):
-        quant("qx", "sx", "xs", H * h, H * h + H)
-    for h in range(2):
-        mx(h, "qv", "sv", 0, "qx", "sx", H * h, H * h + H)
-    store("S", T.oc[:, 0:4 * H], T.qx[:, 0:H].bitcast(dt.uint8), [v("qx", 0, H)])
-    act(v("yo", 0, H), ps(0, 0, H), F_.Copy)
-    copy(v("yo", H, C), ps(1, 0, H))
-    store("S", T.oc[:, 4 * H:4 * C], T.qx[:, H:C].bitcast(dt.uint8), [v("qx", H, C)])
-    store("A", T.y[:, 0:H], T.yo[:, 0:H], [v("yo", 0, H)])
-    for k in range(2):
-        store("S", T.osc[4 * k:4 * k + 4, :], T.sx[32 * k:32 * k + 4, :], [v("sx")])
-    store("S", T.y[:, H:C], T.yo[:, H:C], [v("yo", H, C)])
-    for k in range(2, 4):
-        store("A", T.osc[4 * k:4 * k + 4, :], T.sx[32 * k:32 * k + 4, :], [v("sx")])
+    for k in LAST.split():
+        h = int(k[1])
+        a, z = CUT3[h % 3], CUT3[int(k[3]) if len(k) > 3 else h % 3 + 1]
+        if k[0] == "x":
+            quant("qx", "sx", src[h // 2], a, z)
+        elif k[0] == "m":
+            mx(h, "qv", "sv", 0, "qx", "sx", a, z)
+        elif k[0] == "A":
+            act(v("yo", a, z), ps(h, 0, z - a), F_.Copy)
+        elif k[0] == "V":
+            copy(v("yo", a, z), ps(h, 0, z - a))
+        elif k[0] == "c":
+            store(k[2], T.oc[:, 4 * a:4 * z], T.qx[:, a:z].bitcast(dt.uint8), [v("qx", a, z)])
+        elif k[0] == "y":
+            store(k[2], T.y[:, a:z], T.yo[:, a:z], [v("yo", a, z)])
+        else:
+            store(k[2], T.osc[4 * h:4 * h + 4, :], T.sx[32 * h:32 * h + 4, :], [v("sx")])
 
     needed = set()
     for o in ops:

from concourse.bass import DstId, RemoteDMATransfer
from concourse.mybir import dt, AluOpType, ActivationFunctionType

C, K, ROUNDS = 448, 32, 3
NSEG = C // 16
M = 20
E = 16 * M
CUT3 = (0, 160, 320, 448)
LOADS = "Sx0:320 Ap0:512 Aw0:256 Sw256:512 Ax320:448 Su0:128"
LAYER0 = "x0 x1 m00 m01 m02 m03 E0 E1 A00 V01 A02 V03 m10 m11 m12 m13 x2 A10 y0 A11 V12 A13 u m20 m21 m22 m23 w A20 y1 A21 A22 V23 E2 E3 k"
LAYER = "x0 x1 x2 m00 m01 m02 m03 A00 V01 A02 V03 m10 m11 m12 m13 A10 y0 A11 A12 V13 m20 m21 m22 m23 A20 y1 A21 A22 V23"
ORDER = "y mb ma ha hb da p27 b v20 db p25 p26 qe g10 g14 g11 g12 qd f12 r27 r26 f11 g13 qw11 qr27 f14 p23 f16 p24 f15 r25 f13 p22 g15 r24 r23 qw13 f17 g16 g17 qw15 g18 f18 p21 qr25 qw17 f19 g19 r22 qr23 r21 s20 qw19 qz u e t"
ROWS = "20 27 26 25 24 23 22 z 21"
CUTS = "w11 w13 w15 w17 w19 r27 r25 r23 z"
MOVE = "l1 l2 bt l3 c0:192 s0:192 c192:320 o0:192 s192:320 c320:480 gA0:192 o192:320 s320:480 gV192:320 o320:480"
LATEG = "A0:128"
LAST = "x0 x1 x2 m0 m1 m2 c0S3 s0S s1S s2S s3S A0 V1 V2 y0A3"
BIG = 2.0 ** 90
CODE, F16 = "float8_e4m3fn_x4", "float16"
PRE = 128 - 4 * M
A_ROWS = list(range(NSEG - 1, M - 1, -1))
DS = list(range(M // 2, M))


def layout():
    first = PRE + C // 4
    win = {d: first + 4 * (M + 1) * i for i, d in enumerate(DS)}
    end = first + 4 * (M + 1) * len(DS)
    zero = [(0, PRE), (first, first + 2 * M), (end, end + PRE)] + [(w + 4 * M, w + 4 * M + 4) for w in win.values()]
    row, w, z = {}, end + PRE, {}
    for m in ROWS.split():
        if m[0] == "z":
            zero.append((w, w + PRE))
            z[m], w = w, w + PRE
        else:
            row[int(m)] = w
            w += 4 * int(m)
    chunk, a, name = {}, 0, "d"
    for c in CUTS.split() + ["end"]:
        b = z[c] if c in z else w if c == "end" else (win if c[0] == "w" else row)[int(c[1:])]
        if a < end < b:
            chunk[name] = (a, max(end, a + 128))
            a, name = end, "e"
        chunk[name] = (a, b)
        a, name = b, c
    return win, end, zero, row, w, chunk


WIN, END, ZERO, ROW, NW, CHUNK = layout()

SCRATCH = {
    "x0": ("sbuf", [128, 4 * C], "bfloat16"), "xs": ("sbuf", [128, 4 * C], "bfloat16"), "xl": ("sbuf", [128, 4 * C], "bfloat16"),
    "ys": ("sbuf", [128, 4 * (C + K)], "bfloat16"), "qx": ("sbuf", [128, C], CODE), "sx": ("sbuf", [128, C], "uint8"),
    "wq": ("sbuf", [128, 512], CODE), "wp": ("sbuf", [128, 512], "uint8"),
    "ut": ("sbuf", [128, 512], "bfloat16"), "qu": ("sbuf", [128, 128], CODE), "su": ("sbuf", [128, 128], "uint8"),
    "qus": ("sbuf", [128, 128], CODE), "sus": ("sbuf", [128, 128], "uint8"),
    "vt": ("sbuf", [128, 512], "bfloat16"), "qv": ("sbuf", [128, 128], CODE), "sv": ("sbuf", [128, 128], "uint8"),
    "mm": ("sbuf", [128, C], "float32"), "hh": ("sbuf", [128, C], "float32"), "hb": ("sbuf", [128, E], "float32"),
    "fl": ("sbuf", [128, 4 * NW], "bfloat16"), "qf": ("sbuf", [128, NW], CODE), "sf": ("sbuf", [128, NW], "uint8"),
    "tmp": ("sbuf", [128, 16 * sum(A_ROWS)], "bfloat16"), "acc": ("sbuf", [128, 16], "float32"),
    "a1": ("sbuf", [128, 12 * NSEG], F16), "a2": ("sbuf", [128, 12 * NSEG], F16),
    "offi": ("sbuf", [128, 32], "uint16"), "oo": ("sbuf", [128, C + K], "float32"),
    "g1": ("sbuf", [128, C + K], F16), "g2": ("sbuf", [128, C + K], F16), "offx": ("sbuf", [128, 128], "uint16"),
    "l1": ("sbuf", [128, K], F16), "l2": ("sbuf", [128, K], F16),
    "da": ("sbuf", [128, 2 * C], "bfloat16"), "db": ("sbuf", [128, 2 * C], "bfloat16"),
    "yo": ("sbuf", [128, C], "float32"), "olb": ("sbuf", [128, C], "float32"),
    "pi": ("sbuf", [128, 8], "int32"), "pc": ("sbuf", [128, 16], "float32"),
    "ui": ("sbuf", [128, 8], "int32"), "uoff": ("sbuf", [128, 16], "uint16"),
    "hi": ("sbuf", [128, 32], "int32"), "hoff": ("sbuf", [128, 32], "uint16"),
    "dd": ("sbuf", [128, 516], "bfloat16"), "ce": ("sbuf", [128, 516], "bfloat16"), "dabs": ("sbuf", [128, 512], "bfloat16"),
    "cv": ("sbuf", [128, 32], "bfloat16"), "ct": ("sbuf", [128, 1024], "bfloat16"),
    "qc": ("sbuf", [128, 6 * 128], CODE), "sc": ("sbuf", [128, 6 * 128], "uint8"),
    "n16": ("sbuf", [128, C], "bfloat16"), "n4": ("sbuf", [128, C + K], "bfloat16"), "n8": ("sbuf", [128, K], "bfloat16"),
    "n12": ("sbuf", [128, 12 * NSEG], "bfloat16"), "keep12": ("sbuf", [128, 12 * NSEG], "bfloat16"),
    "maska": ("sbuf", [128, C], "bfloat16"), "cseg": ("sbuf", [128, C], "bfloat16"),
    "keep4": ("sbuf", [128, C + K], "bfloat16"), "mask4": ("sbuf", [128, C + K], "bfloat16"),
    "keep8": ("sbuf", [128, K], "bfloat16"), "mask8": ("sbuf", [128, K], "bfloat16"),
    "jj": ("sbuf", [128, C], "float32"), "kio": ("sbuf", [128, 32], "float32"), "zt": ("sbuf", [128, 256], "bfloat16"),
}
for _t in range(ROUNDS):
    SCRATCH["qy%d" % _t] = ("sbuf", [128, C], CODE)
    SCRATCH["sy%d" % _t] = ("sbuf", [128, C], "uint8")
    SCRATCH["lq%d" % _t] = ("sbuf", [128, C], CODE)
    SCRATCH["lp%d" % _t] = ("sbuf", [128, C], "uint8")
    SCRATCH["lo%d" % _t] = ("sbuf", [128, 16], "uint16")
    SCRATCH["ll%d" % _t] = ("sbuf", [128, 16], "uint16")
for _b in range(8):
    SCRATCH["ps%d" % _b] = ("psum", [128, 512], "float32")

SEMAPHORES = (["sV", "sA", "sP", "sG", "st", "left"] + ["ld%d" % i for i in range(9)]
              + ["%s%d" % (s, t) for s in ("ra", "rl", "ba", "la") for t in range(ROUNDS)])

A_, F_ = AluOpType, ActivationFunctionType


def bits(engines):
    return sum(1 << e for e in engines)


def relays(T, topo, r):
    src, dst = T.cores[r], T.cores[(r - 1) % len(T.cores)]
    can = [d for d in topo.cores_of(src) if d != src and topo.may_write(d, dst)]
    return sorted(can, key=lambda d: (topo.die(d) != topo.die(src), d))[:4], dst


def pieces(t):
    q = C // 4
    return [("qy%d" % t, "lq%d" % t, q * i, q * i + q, i) for i in range(4)] + [("sy%d" % t, "lp%d" % t, 0, C, 2)]


def side(T, name, a, b):
    v = T[name][:, a:b]
    return v.bitcast(dt.uint8) if SCRATCH[name][2] == CODE else v


def relay_program(g, core, T, topo):
    for r, c in enumerate(T.cores):
        if core in topo.cores_of(c):
            rel, dst = relays(T, topo, r)
            if core not in rel:
                return
            k = rel.index(core)
            on, off = topo.engines(c, core), topo.engines(core, dst)
            rid, pid = topo.addr(dst, core)
            for t in range(ROUNDS):
                mine = [p for p in pieces(t) if p[4] == k]
                g.wait_ge(T.sem["ra%d" % t], len(on) // 4 + (len(mine) - 1) * len(on))
                e = len(off) // len(mine)
                g.remote_dma_fused([RemoteDMATransfer(dst_ids=[DstId(rid=rid, pnc=pid)], dma_engine_mask=bits(off[e * i:e * i + e]),
                                                      remote_sem=T.sem["ba%d" % t], src=side(T, p[1], p[2], p[3]), dst=side(T, p[1], p[2], p[3]))
                                    for i, p in enumerate(mine)], local_sem=T.sem.left)
                if k == 0:
                    g.wait_ge(T.sem["rl%d" % t], len(on))
                    g.remote_dma(T["ll%d" % t][:, 0:4], T["ll%d" % t][:, 0:4], T.sem["la%d" % t], T.sem.left, pid, rid, bits(off))
            g.wait_ge(T.sem.left, ROUNDS * len(off) * (2 if k == 0 else 1))
            return


def rank_program(g, core, T, topo):
    rank = T.rank_of(core)
    if rank is None:
        relay_program(g, core, T, topo)
        return
    rel, _ = relays(T, topo, rank)
    eng = {"V": g.vector, "A": g.scalar, "P": g.tensor, "G": g, "S": g.sync}
    ops, hist, masks = [], {}, {}

    def v(name, a=0, b=None, step=1):
        return (name, a, SCRATCH[name][1][1] if b is None else b, step)

    def ap(x):
        return T[x[0]][:, x[1]:x[2]:x[3]] if x[3] != 1 else T[x[0]][:, x[1]:x[2]]

    def span(x):
        if SCRATCH[x[0]][0] == "psum":
            return 1
        if x[1:] not in masks:
            masks[x[1:]] = sum(1 << i for i in range(x[1], x[2], x[3]))
        return masks[x[1:]]

    def op(e, fn, reads, writes, sem=None, val=None):
        me, deps = len(ops), set()
        for x, wr in [(x, False) for x in reads] + [(x, True) for x in writes]:
            m, psum = span(x), SCRATCH[x[0]][0] == "psum"
            for o, om, ow in hist.get(x[0], []):
                if om & m and o != me:
                    same = ops[o]["e"] == e
                    if (psum and same and e == "P") or not (wr or ow or (psum and not same)):
                        continue
                    deps.add(o)
            hist[x[0]] = [h for h in hist.get(x[0], []) if not (wr and h[1] & ~m == 0)] + [(me, m, wr)]
        ops.append({"e": e, "fn": fn, "deps": deps, "sem": sem, "val": val})

    def ts(out, in0, s1, op0, s2=None, op1=None):
        rd = [in0] + [s for s in (s1, s2) if isinstance(s, tuple)]
        a1, a2 = [ap(s) if isinstance(s, tuple) else s for s in (s1, s2)]
        if op1 is None:
            op("V", lambda q: q.tensor_scalar(ap(out), ap(in0), a1, None, op0), rd, [out])
        else:
            op("V", lambda q: q.tensor_scalar(ap(out), ap(in0), a1, a2, op0, op1), rd, [out])

    def tt(out, in0, in1, o):
        op("V", lambda q: q.tensor_tensor(ap(out), ap(in0), ap(in1), o), [in0, in1], [out])

    def scan(out, d0, d1, o0, o1):
        op("V", lambda q: q.tensor_tensor_scan(ap(out), ap(d0), ap(d1), 0.0, o0, o1), [d0, d1], [out])

    def copy(out, in_):
        op("V", lambda q: q.tensor_copy(ap(out), ap(in_)), [in_], [out])

    def fill(out, c):
        op("V", lambda q: q.memset(ap(out), c), [], [out])

    def act(out, in_, f, bias=None, scale=None, accum=None):
        kw = {}
        if bias is not None:
            kw["bias"] = ap(bias) if isinstance(bias, tuple) else bias
        if scale is not None:
            kw["scale"] = scale
        if accum is not None:
            kw["accum_out"] = ap(accum)
        op("A", lambda q: q.activation(ap(out), ap(in_), f, **kw), [in_] + ([bias] if isinstance(bias, tuple) else []),
           [out] + ([accum] if accum else []))

    def gather(e, out, win, off):
        if e == "V":
            op(e, lambda q: q.tensor_copy(ap(out), ap(win).indirect(ap(off))), [win, off], [out])
        else:
            op(e, lambda q: q.activation(ap(out), ap(win).indirect(ap(off)), F_.Copy), [win, off], [out])

    def scatter(win, off, in_):
        op("V", lambda q: q.tensor_copy(ap(win).indirect(ap(off)), ap(in_)), [in_, off], [win])

    def quant(q, s, src, a, b, at=None):
        i = v(src, 4 * a, 4 * b) if at is None else v(src, at, at + 4 * (b - a))
        op("V", lambda e: e.quantize_mx(ap(v(q, a, b)), ap(v(s, a, b)), ap(i)), [i], [v(q, a, b), v(s, a, b)])

    def mx(bank, lq, ls, la, rq, rs, a, b, start=True, stop=True):
        out = v("ps%d" % bank, 0, b - a)
        rd = [v(lq, la, la + 128), v(ls, la, la + 128), v(rq, a, b), v(rs, a, b)]
        op("P", lambda e: e.matmul_mx(ap(out), ap(rd[0]), ap(rd[1]), ap(rd[2]), ap(rd[3]), start, stop), rd, [out])

    def iota(out, pattern, base, cm):
        if SCRATCH[out[0]][2] == "int32":
            op("G", lambda q: q.iota(ap(out), pattern, base, cm), [], [out])
        else:
            op("G", lambda q: q.iota(ap(out), pattern, base, cm, allow_small_or_imprecise_dtypes=True), [], [out])

    loads, stores = [0], [0]

    def load(e, out, src, after=()):
        o = ap(out).bitcast(dt.uint8) if SCRATCH[out[0]][2] == CODE else ap(out)
        op(e, lambda q: q.dma_start(o, src), list(after), [out], sem="ld%d" % loads[0], val=16)
        loads[0] += 1

    def store(e, dst, src, reads):
        op(e, lambda q: q.dma_start(dst, src), reads, [], sem="st", val=16)
        stores[0] += 1

    def ps(b, a, c):
        return v("ps%d" % b, a, c)

    def col(name, j):
        return v(name, j, j + 1)

    for k in LOADS.split():
        a, b = [int(i) for i in k[2:].split(":")]
        name, whole, n = {"x": ("x0", T.x, 4), "w": ("wq", T.wc, 4), "p": ("wp", T.ws, 1), "u": ("ut", T.u, 4)}[k[1]]
        load(k[0], v(name, a, b) if k[1] in "wp" else v(name, 4 * a, 4 * b), whole[:, n * a:n * b])

    iota(col("pi", 0), [[0, 1]], 0, 1)
    iota(v("dd"), [[1, 516]], -3, -4)
    iota(v("cv"), [[1, 8], [0, 4]], 0, 0)
    iota(v("n16"), [[0, NSEG], [1, 16]], 0, 0)
    iota(v("ui"), [[16, 8]], 0, 0)
    iota(v("hi", 0, M), [[16, M]], 15, 0)
    iota(v("kio", 0, M), [[16, 2], [0, M // 2]], 16 * len(DS) - 16, 0)
    iota(v("kio", M, NSEG), [[16, NSEG - M]], 16 * M, 0)
    iota(v("n4"), [[0, (C + K) // 4], [1, 4]], 0, 0)
    iota(v("n8"), [[0, K // 8], [1, 8]], 0, 0)
    fill(v("zt"), 0.0)
    for j, (sh, msk) in enumerate([(0, 15), (4, 7), (2, 3), (0, 3), (1, 7), (0, 1)]):
        ts(col("pi", j + 1), col("pi", 0), sh, A_.logical_shift_right, msk, A_.bitwise_and)
    fill(v("ct", 512, 1024), 0.0)
    copy(v("pc", 0, 6), v("pi", 1, 7))
    copy(v("a1", 2, 12 * NSEG, 3), v("zt", 0, 4 * NSEG))
    fill(v("ys", 4 * C, 4 * (C + K)), 0.0)
    p_r, p_g, p_r4, p_t, p_r2, p_h, p_nb = [col("pc", j) for j in range(7)]
    for a, b in ZERO:
        act(v("fl", 4 * a, 4 * b), v("zt", 0, 4 * (b - a)), F_.Copy)
    ts(p_nb, p_r, -BIG, A_.mult)
    act(v("dabs"), v("dd", 3, 515), F_.Abs, bias=-1.5)
    ts(v("ce"), v("dd"), 0.0, A_.is_equal)
    for t in range(4):
        ts(v("ct", 512 + 5 * t, 1024, 16), v("cv"), p_g, A_.is_equal, -1.0, A_.mult)
    ts(v("ct", 0, 512), v("dabs"), 2.0, A_.is_lt)
    act(v("maska"), v("n16"), F_.Abs, bias=p_nb, scale=BIG)
    act(v("cseg"), v("n16"), F_.Relu, bias=BIG, scale=-BIG)
    quant("qc", "sc", "ct", 512, 768, 0)
    copy(v("uoff", 0, 8), v("ui"))
    copy(v("hoff", 0, M), v("hi", 0, M))
    src = ("x0", "x0")

    for t in range(ROUNDS):
        qy, sy = "qy%d" % t, "sy%d" % t
        for k in (LAYER if t else LAYER0).split():
            if k == "u":
                quant("qu", "su", "ut", 0, 128)
            elif k == "w":
                op("V", lambda q: q.tensor_copy(T.qus[:, 0:128].bitcast(dt.uint32), T.qu[:, 0:128].bitcast(dt.uint32).indirect(T.uoff[:, 0:8])),
                   [v("qu"), v("uoff", 0, 8)], [v("qus")])
                gather("A", v("sus"), v("su"), v("uoff", 0, 8))
            elif k == "k":
                ts(v("mask4"), v("n4"), p_r4, A_.is_equal)
                ts(v("a1", 2, 12 * NSEG, 12), v("kio", 0, NSEG), p_r, A_.add)
            elif k[0] == "E":
                b = int(k[1])
                quant("qc", "sc", "ce", 128 * b, 128 * b + 128, 3 - b)
            else:
                h = int(k[1])
                a, z = CUT3[h], CUT3[h + 1]
                if k[0] == "x":
                    quant("qx", "sx", src[h // 2], a, z)
                elif k[0] == "y":
                    quant(qy, sy, "ys", a, z)
                else:
                    b = int(k[2])
                    bank, out = b + 4 * (1 - h % 2), v("ys", 4 * a + b, 4 * z, 4)
                    if k[0] == "m":
                        mx(bank, "wq", "wp", 128 * b, "qx", "sx", a, z)
                    elif k[0] == "V":
                        ts(out, ps(bank, 0, z - a), 0.03125, A_.mult)
                    else:
                        act(out, ps(bank, 0, z - a), F_.Copy, scale=0.03125)
        mx(0, "qus", "sus", 0, qy, sy, 0, E)
        pcs = pieces(t)
        on = topo.engines(core, rel[0])
        e4 = len(on) // 4

        def send_codes(q, pcs=pcs, t=t):
            tr = []
            for i, p in enumerate(pcs[:4]):
                rid, pid = topo.addr(rel[p[4]], core)
                tr.append(RemoteDMATransfer(dst_ids=[DstId(rid=rid, pnc=pid)], dma_engine_mask=bits(on[e4 * i:e4 * i + e4]),
                                            remote_sem=T.sem["ra%d" % t], src=side(T, p[0], p[2], p[3]), dst=side(T, p[1], p[2], p[3])))
            q.remote_dma_fused(tr, local_sem=T.sem.left)

        def send_scales(q, p=pcs[4], t=t):
            rid, pid = topo.addr(rel[p[4]], core)
            q.remote_dma(side(T, p[1], p[2], p[3]), side(T, p[0], p[2], p[3]), T.sem["ra%d" % t], T.sem.left, pid, rid, bits(on))

        t0 = {m: 16 * sum(a for a in A_ROWS if a > m) for m in A_ROWS}
        sums = [("c", PRE, C // 4), ("w", PRE, C // 4)] + [("c", WIN[d], 4 * M) for d in DS] + [("c", ROW[m], 4 * m) for m in A_ROWS]
        sums += [("w", END - 4 * M * i, 4 * M) for i in range(1, len(DS) + 1)]
        have, begun = set(), set()
        for k in ORDER.split():
            m = int(k[1:]) if k[1:].isdigit() else 0
            a, b = (E, C) if k[1:] == "a" else (0, E)
            score = ps(5, 0, C - E) if a else ps(0, 0, E)
            if k == "y":
                quant(qy, sy, "ys", E, C)
                mx(5, "qus", "sus", 0, qy, sy, E, C)
                mx(1, "qus", "sus", 0, qy, sy, 0, C)
                op("G", send_codes, [v(qy)], [], sem="")
                op("G", send_scales, [v(sy)], [], sem="")
                if t == 0:
                    act(v("keep8"), v("n8"), F_.Sign)
                    act(v("keep4"), v("n4"), F_.Sign)
                    iota(v("n12"), [[0, NSEG], [1, 12]], 0, 0)
                    iota(v("jj"), [[4, C]], 0, 0)
                    iota(v("oo", C, C + K), [[4, K]], 4 * C, 0)
            elif k[0] == "m":
                tt(v("mm", a, b), score, v("maska", a, b), A_.add)
            elif k[0] == "h":
                scan(v("hh", a, b), v("cseg", a, b), v("mm", a, b), A_.add, A_.min)
            elif k == "b":
                gather("A", v("hb"), v("hh", 0, E), v("hoff", 0, M))
            elif k[0] == "d":
                tt(v("fl", 4 * PRE + a, 4 * PRE + b), score, v("hh", a, b), A_.is_gt)
            elif k[0] in "fg":
                w, n = 4 * WIN[m], 16 * (M - m)
                if k[0] == "f":
                    tt(v("fl", w, w + n), ps(0, 0, n), v("hb", E - n, E), A_.is_ge)
                else:
                    tt(v("fl", w + n, w + E), ps(0, n, E), v("hb", 0, E - n), A_.is_gt)
            elif k[0] in "vspr":
                row, mid, own = v("fl", 4 * ROW[m], 4 * ROW[m] + 16 * m), v("tmp", t0[m], t0[m] + 16 * m), col("hh", 16 * m + 15)
                if k[0] == "v":
                    ts(row, ps(0, 0, 16 * m), own, A_.is_lt, -1.0, A_.mult)
                elif k[0] == "s":
                    act(mid, row, F_.Copy, accum=col("acc", m - M))
                elif k[0] == "p":
                    act(mid, ps(1, 0, 16 * m), F_.Relu, bias=own, scale=-1.0)
                else:
                    act(row, mid, F_.Sign, scale=-1.0, accum=col("acc", m - M))
            elif k == "u":
                copy(v("a1", 12 * M + 5, 12 * NSEG, 12), v("acc", 0, NSEG - M))
            elif k == "e":
                copy(v("a1", 1, 12 * NSEG, 3), ps(3, PRE, PRE + C // 4))
            elif k == "t":
                if t == 0:
                    ts(v("keep12"), v("n12"), 0.5, A_.is_gt)
                tt(v("a1", 0, 12 * NSEG, 3), ps(2, PRE, PRE + C // 4), v("mask4", 0, C // 4), A_.mult)
            else:
                quant("qf", "sf", "fl", *CHUNK[k[1:]])
                have |= set(range(*CHUNK[k[1:]]))
                for x in sorted(sums, key=lambda x: (x[0] == "c", x[1])):
                    if all(w in have for w in range(x[1] - PRE, x[1] + x[2])) and (x[0] in begun or x[1] == PRE):
                        sums.remove(x)
                        c = x[0] == "c"
                        mx(2 if c else 3, "qc", "sc", 640 if c else 512, "qf", "sf", x[1] - PRE, x[1] + x[2],
                           x[0] not in begun, all(y[0] != x[0] for y in sums))
                        begun.add(x[0])
        scan(v("a2"), v("keep12"), v("a1"), A_.mult, A_.add)
        if t == 0:
            ts(v("mask8"), v("n8"), p_r2, A_.is_equal)
        copy(v("offi", 0, NSEG), v("a2", 11, 12 * NSEG, 12))
        scatter(v("oo", 0, C), v("offi", 0, NSEG), v("jj"))
        nxt = (rank + 1) % len(T.cores)
        noff = len(topo.engines(relays(T, topo, nxt)[0][0], core))
        op("X", None, [], [v("lq%d" % t), v("lp%d" % t)], sem="ba%d" % t, val=4 * noff)
        for b in range(4):
            mx(4 + b, "qc", "sc", 128 * b, "lq%d" % t, "lp%d" % t, 0, C)
        if t == 1:
            load("S", v("vt"), T.v[:], after=[v("lq1")])
        for b in range(4):
            act(v("db" if b % 2 else "da", b // 2, 2 * C, 2), ps(4 + b, 0, C), F_.Copy)
        if t == ROUNDS - 1:
            act(v("olb"), v("oo", 0, C), F_.Copy, scale=0.25)
            for k in range(8):
                store("S", T.ol[k:k + 1, :], T.olb[16 * k:16 * k + 1, :], [v("olb")])
        lo = v("lo%d" % t, 0, 4)

        def send_list(q, t=t):
            rid, pid = topo.addr(rel[0], core)
            q.remote_dma(T["ll%d" % t][:, 0:4], T["lo%d" % t][:, 0:4], T.sem["rl%d" % t], T.sem.left, pid, rid, bits(on))

        def composed(a, b):
            op("V", lambda q: q.tensor_tensor(ap(v("g1", a, b)), ap(v("oo", K, C + K)).indirect(ap(v("offi", a // 16, b // 16))),
                                              ap(v("mask4", a, b)), A_.mult),
               [v("oo", K, C + K), v("offi", a // 16, b // 16), v("mask4", a, b)], [v("g1", a, b)])
        for k in MOVE.split():
            if k == "l1":
                tt(v("l1"), v("oo", 0, K), v("mask8"), A_.mult)
            elif k == "l2":
                scan(v("l2"), v("keep8"), v("l1"), A_.mult, A_.add)
            elif k == "l3":
                ts(lo, v("l2", 7, K, 8), 0.5, A_.mult, p_h, A_.add)
                op("G", send_list, [lo], [], sem="")
            elif k == "bt":
                tt(v("g1", C, C + K), v("oo", C - K, C), v("mask4", 0, K), A_.mult)
            else:
                a, b = [int(x) for x in k.lstrip("csogAV").split(":")]
                if k[0] == "c":
                    composed(a, min(b, C))
                elif k[0] == "s":
                    scan(v("g2", a, b), v("keep4", a, b), v("g1", a, b), A_.mult, A_.add)
                elif k[0] == "o":
                    ts(v("offx", a // 4, b // 4), v("g2", a + 3, b, 4), p_t, A_.add)
                else:
                    gather(k[1], v("xs", 4 * a, 4 * b), v("ys"), v("offx", a // 4, b // 4))
        if t == ROUNDS - 1:
            quant("qv", "sv", "vt", 0, 128)
        ll = v("ll%d" % t, 0, 4)
        op("X", None, [], [ll], sem="la%d" % t, val=noff)
        gather("V", v("ys", 4 * C, 4 * (C + K), 2), v("da"), ll)
        gather("A", v("ys", 4 * C + 1, 4 * (C + K), 2), v("db"), ll)
        scatter(v("xs"), v("offx", C // 4, (C + K) // 4), v("ys", 4 * C, 4 * (C + K)))
        for k in LATEG.split():
            a, b = [E + int(x) for x in k[1:].split(":")]
            gather(k[0], v("xl", 4 * a, 4 * b), v("ys"), v("offx", a // 4, b // 4))
        src = ("xs", "xl")

    for k in LAST.split():
        h = int(k[1])
        a, z = CUT3[h % 3], CUT3[int(k[3]) if len(k) > 3 else h % 3 + 1]
        if k[0] == "x":
            quant("qx", "sx", src[h // 2], a, z)
        elif k[0] == "m":
            mx(h, "qv", "sv", 0, "qx", "sx", a, z)
        elif k[0] == "A":
            act(v("yo", a, z), ps(h, 0, z - a), F_.Copy)
        elif k[0] == "V":
            copy(v("yo", a, z), ps(h, 0, z - a))
        elif k[0] == "c":
            store(k[2], T.oc[:, 4 * a:4 * z], T.qx[:, a:z].bitcast(dt.uint8), [v("qx", a, z)])
        elif k[0] == "y":
            store(k[2], T.y[:, a:z], T.yo[:, a:z], [v("yo", a, z)])
        else:
            store(k[2], T.osc[4 * h:4 * h + 4, :], T.sx[32 * h:32 * h + 4, :], [v("sx")])

    needed = set()
    for o in ops:
        needed |= o["deps"]
    count = {}
    for i, o in enumerate(ops):
        if o["sem"] is None and i in needed:
            o["sem"] = "s" + o["e"]
            count[o["sem"]] = o["val"] = count.get(o["sem"], 0) + 1
            o["inc"] = 1
        elif o["sem"] and o["fn"]:
            o["inc"] = 16
    seen = {e: {} for e in eng}
    for o in ops:
        if o["fn"] is None:
            continue
        want = {}
        for d in o["deps"]:
            s = ops[d]["sem"]
            if s:
                want[s] = max(want.get(s, 0), ops[d]["val"])
        for s in sorted(want):
            if seen[o["e"]].get(s, 0) < want[s]:
                eng[o["e"]].wait_ge(T.sem[s], want[s])
                seen[o["e"]][s] = want[s]
        ins = o["fn"](eng[o["e"]])
        if "inc" in o:
            ins.then_inc(T.sem[o["sem"]], o["inc"])
    g.sync.wait_ge(T.sem.st, 16 * stores[0])
    g.wait_ge(T.sem.left, ROUNDS * 3 * len(topo.engines(core, rel[0])))
